import numpy as np, ml_dtypes
CORES = [16,32,48,64,80]
N = 5
import mx_ref
BF = ml_dtypes.bfloat16
def entries(a):
    return np.ascontiguousarray(a.T).reshape(-1)
def table(e):
    return np.ascontiguousarray(np.reshape(e, (-1, 16)).T).astype(np.int32)
def gpick(z, e):
    return np.concatenate([z[16 * g:16 * g + 16][:, e[g]] for g in range(8)])
def tile(rs):
    return np.stack(rs, axis=2).reshape(128, -1).astype(BF)
def cut(t, i, w=512):
    return t[:, w * i:w * i + w]
def f(rng, *shape):
    return mx_ref.flush((rng.standard_normal(shape, dtype=np.float32) * np.exp2(rng.integers(-2, 3, shape[:-1] + (1,)))).astype(BF))
def wide(rng, *shape, cols=0):
    v = rng.standard_normal(shape, dtype=np.float32) * np.exp2(rng.integers(-12, 13, shape)).astype(np.float32)
    if cols: v *= np.repeat(np.exp2(rng.integers(-cols, cols + 1, shape[:-2] + (1, shape[-1] // 4))) * (rng.random(shape[:-2] + (1, shape[-1] // 4)) > 0.0625), 4, axis=-1).astype(np.float32)
    return mx_ref.flush(v.astype(BF))
TQ, O = 384, 1
def lay(k, q):
    return {"kp": np.repeat(k, 16, axis=1).astype(np.int32), "qp": np.stack([table(e) for e in q])}
def setup_inputs(rng):
    d = {"qx": f(rng, N, 128, 4 * TQ), "ky": f(rng, N, 128, 2048), "rt": np.repeat(f(rng, 1, 128, 1024), N, axis=0), "vv": f(rng, N, 128, 512 * O)}
    a = rng.integers(0, 3585)
    k = a + rng.integers(0, 512, (N, 8, 4))
    q = np.where(rng.random((N, TQ)) < 0.25, rng.integers(0, 4096, (N, TQ)), a + rng.integers(0, 512, (N, TQ)))
    return {**d, **lay(k, q)}
def setup_inputs_far(rng):
    d = setup_inputs(rng)
    k = rng.integers(1500, 2501, (N, 32)); q = np.zeros((N, TQ), int); a = int(rng.integers(0, 2))
    for r in range(N):
        k[r, rng.permutation(32)[:2]] = [1500, 2500]
        lo, hi = (2628, 4095) if (r + a) % 2 else (0, 1371)
        q[r] = rng.integers(lo, hi + 1, TQ)
        q[r, rng.permutation(TQ)[:2]] = [lo, hi]
    return {**d, **lay(k.reshape(N, 8, 4), q)}
def setup_inputs_same(rng):
    d = setup_inputs(rng); a = int(rng.integers(0, 4096))
    return {**d, **lay(np.full((N, 8, 4), a), np.full((N, TQ), a))}
def setup_inputs_descending(rng):
    d = setup_inputs(rng); a = rng.integers(0, 3585)
    q = np.stack([a + np.sort(rng.permutation(512)[:TQ])[::-1] for r in range(N)])
    k = np.stack([a + 16 * rng.permutation(32) + rng.integers(0, 16, 32) for r in range(N)])
    return {**d, **lay(k.reshape(N, 8, 4), q)}
def setup_inputs_near(rng):
    d = setup_inputs(rng); a = rng.integers(2049, 3968)
    q = np.stack([a + rng.permutation(TQ) % 128 for r in range(N)])
    k = np.stack([a + rng.permutation(np.concatenate([[0, 128], 1 + rng.permutation(127)[:30]])) for r in range(N)])
    return {**d, **lay(k.reshape(N, 8, 4), q)}
def setup_inputs_spread(rng):
    d = setup_inputs(rng); d["qx"] = wide(rng, N, 128, 4 * TQ, cols=4); return d
def check_inputs(d):
    b = []
    for r in range(N):
        k, q = d["kp"][r], entries(d["qp"][r])
        if d["rt"][r].tobytes() != d["rt"][0].tobytes(): b.append("rt")
        if k.min() < 0 or k.max() > 4095 or (k != np.repeat(k[::16], 16, axis=0)).any(): b.append("kp")
        if q.min() < 0 or q.max() > 4095: b.append("qp")
    return b
def reference(qx, ky, rt, vv, kp, qp):
    y = np.zeros((N, 128, O * TQ), np.float32)
    X = [mx_ref.quantize(qx[r]) for r in range(N)]
    for s in range(N):
        K = [mx_ref.quantize(np.ascontiguousarray(cut(ky[s], b))) for b in range(4)]
        V = [mx_ref.quantize(np.ascontiguousarray(cut(vv[s], o))) for o in range(O)]
        R = mx_ref.quantize(rt[s])
        P = [mx_ref.matmul(K[b], R) for b in range(4)]
        for r in range(N):
            A = []
            for b in range(4):
                c = np.clip(entries(qp[r])[None, :] - kp[s][::16, b][:, None], -128, 127) + 128
                A.append(np.maximum(mx_ref.matmul(K[b], X[r]) + gpick(P[b], c), np.float32(0)) * np.float32(0.03125))
            A = mx_ref.quantize(tile(A))
            for o in range(O): y[r][:, TQ * o:TQ * o + TQ] += mx_ref.matmul(V[o], A)
    return {"y": y}

@@ -1,0 +1,321 @@
+from concourse.bass import DstId, RemoteDMATransfer
+from concourse.mybir import dt, AluOpType, ActivationFunctionType
+
+N = 5
+TQ = 384
+RT = 256
+XW = TQ + RT
+HALF = TQ // 2
+
+SCRATCH = {
+    "kyb": ("sbuf", [128, 2048], "bfloat16"),
+    "qxb": ("sbuf", [128, 4 * TQ], "bfloat16"),
+    "rtb": ("sbuf", [128, 4 * RT], "bfloat16"),
+    "vvb": ("sbuf", [128, 512], "bfloat16"),
+    "ko": ("sbuf", [128, 512], "float8_e4m3fn_x4"),
+    "kos": ("sbuf", [128, 512], "uint8"),
+    "kw": ("sbuf", [128, 128], "float8_e4m3fn_x4"),
+    "kc": ("sbuf", [128, 512], "float8_e4m3fn_x4"),
+    "kcs": ("sbuf", [128, 512], "uint8"),
+    "xc": ("sbuf", [128, XW], "float8_e4m3fn_x4"),
+    "xs": ("sbuf", [128, XW], "uint8"),
+    "vo": ("sbuf", [128, 128], "float8_e4m3fn_x4"),
+    "vos": ("sbuf", [128, 128], "uint8"),
+    "vr": ("sbuf", [128, 512], "float8_e4m3fn_x4"),
+    "vrs": ("sbuf", [128, 512], "uint8"),
+    "ar": ("sbuf", [128, 3 * TQ], "float8_e4m3fn_x4"),
+    "ars": ("sbuf", [128, 3 * TQ], "uint8"),
+    "kpo": ("sbuf", [128, 4], "int32"),
+    "kpf": ("sbuf", [128, 4], "int32"),
+    "kpr": ("sbuf", [128, 4], "int32"),
+    "qr": ("sbuf", [128, 24], "int32"),
+    "ysb": ("sbuf", [128, TQ], "float32"),
+}
+BANKS = ["pb0", "pb1", "yb0", "yb1", "sb0", "sb1", "sb2", "sb3"]
+for _n in BANKS:
+    SCRATCH[_n] = ("psum", [128, 512], "float32")
+for _u in range(2):
+    SCRATCH["kf%d" % _u] = ("sbuf", [128, 4], "float32")
+    SCRATCH["ot%d" % _u] = ("sbuf", [128, 96], "float32")
+    SCRATCH["om%d" % _u] = ("sbuf", [128, 96], "float32")
+    SCRATCH["off%d" % _u] = ("sbuf", [128, 96], "uint16")
+    SCRATCH["pw%d" % _u] = ("sbuf", [128, 4 * RT], "float32")
+    SCRATCH["pk%d" % _u] = ("sbuf", [128, 4 * TQ], "float32")
+    SCRATCH["at%d" % _u] = ("sbuf", [128, 4 * TQ], "bfloat16")
+    SCRATCH["ac%d" % _u] = ("sbuf", [128, TQ], "float8_e4m3fn_x4")
+    SCRATCH["as%d" % _u] = ("sbuf", [128, TQ], "uint8")
+
+SEMAPHORES = ["l_k0", "l_k1", "l_rt", "l_qx", "l_vv", "l_kp", "l_qp",
+              "q_k0", "q_k1", "q_rt", "q_qx", "q_vv",
+              "r_kpf", "r_kp", "r_kw", "r_k0", "r_k1", "r_k2", "r_k3", "r_ks", "r_x", "r_q",
+              "r_vc", "r_vs", "r_v1", "r_v2", "r_v3", "r_v4", "r_a10", "r_a11", "r_a20", "r_a21", "r_a30", "r_a31",
+              "sent", "m_y0", "m_y1", "c_y0", "c_y1", "st0", "st1"]
+for _u in range(2):
+    SEMAPHORES += ["%s%d" % (_n, _u) for _n in ("o_k", "o_t", "o_m", "o_o", "rb")]
+    SEMAPHORES += ["%s%d%d" % (_n, _u, _h) for _n in ("rl", "qa") for _h in range(2)]
+    SEMAPHORES += ["%s%d%d" % (_n, _u, _b) for _n in ("m_p", "m_s", "c_p") for _b in range(4)]
+    SEMAPHORES += ["%s%d%d%d" % (_n, _u, _b, _h) for _n in ("ga", "ad") for _b in range(4) for _h in range(2)]
+
+
+def bits(es):
+    return sum(1 << e for e in es)
+
+
+def team(rank_core, topo):
+    mine = topo.cores_of(rank_core)
+    near = [c for c in mine if c != rank_core and topo.die(c) == topo.die(rank_core)]
+    far = [c for c in mine if topo.die(c) != topo.die(rank_core)]
+    return near[:3], far
+
+
+def rank_program(g, core, T, topo):
+    v, sc, pe, sy = g.vector, g.scalar, g.tensor, g.sync
+    cores = list(T.cores)
+    teams = [team(c, topo) for c in cores]
+    r = None
+    for i, c in enumerate(cores):
+        if core == c or core in teams[i][0] or core in teams[i][1]:
+            r = i
+    if r is None:
+        return
+    me = cores[r]
+    near, far = teams[r]
+    relays = [far[0], near[0], far[1], near[1]]
+    posts = [far[0], near[0], near[2], near[1]]
+    out = topo.engines(me, cores[(r + 1) % N])
+    every = topo.engines(me, far[0])
+    stay = [e for e in every if e not in out]
+    few = len(stay) // 2
+    sent = [0]
+
+    def worker(s, d):
+        i = (s + d) % N
+        return teams[i][0][d - 1] if d < 4 else cores[i]
+
+    users = [worker(r, d) for d in (1, 2, 3, 4)]
+
+    def wait(queue, name, n=1):
+        queue.wait_ge(T.sem[name], n)
+
+    def inc(ins, name, n=1):
+        ins.then_inc(T.sem[name], n)
+
+    def move(dsts, outs, src, sem, es):
+        ids = []
+        for c in dsts:
+            a = topo.addr(c)
+            ids.append(DstId(rid=a[0], pnc=a[1]))
+        sent[0] += len(es)
+        return RemoteDMATransfer(dst_ids=ids, dma_engine_mask=bits(es), remote_sem=T.sem[sem], srcs=[src], dsts=list(outs))
+
+    def send(*moves):
+        g.remote_dma_fused(list(moves), local_sem=T.sem["sent"])
+
+    def by(t):
+        return t.bitcast(dt.uint8)
+
+    def offsets(u, kp, kp_event, q_event):
+        kf, ot, om, off = T["kf%d" % u], T["ot%d" % u], T["om%d" % u], T["off%d" % u]
+        wait(v, *kp_event)
+        inc(v.tensor_copy(kf[:], kp[:]), "o_k%d" % u)
+        wait(v, *q_event)
+        wait(v, "o_k%d" % u)
+        for b in range(4):
+            inc(v.tensor_scalar(ot[:, 24 * b:24 * b + 24], T.qr[:], kf[:, b:b + 1], -128.0, AluOpType.subtract, AluOpType.max), "o_t%d" % u)
+        wait(v, "o_t%d" % u, 4)
+        inc(v.tensor_scalar(om[:], ot[:], 127.0, 128.0, AluOpType.min, AluOpType.add), "o_m%d" % u)
+        wait(v, "o_m%d" % u)
+        inc(v.tensor_copy(off[:], om[:]), "o_o%d" % u)
+
+    def products(u, kc, ks, banks, events, events_x):
+        for h in range(2):
+            for b in (2 * h, 2 * h + 1):
+                for e in events[b]:
+                    wait(pe, *e)
+                if b >= banks:
+                    wait(pe, "c_p%d%d" % (u, b - banks))
+                elif u:
+                    wait(pe, "c_p%d%d" % (u - 1, b))
+                    wait(pe, "c_p%d%d" % (u - 1, b + 2))
+                inc(pe.matmul_mx(T[BANKS[b % banks]][:, 0:RT], kc[:, 128 * b:128 * b + 128], ks[:, 128 * b:128 * b + 128],
+                                 T.xc[:, TQ:XW], T.xs[:, TQ:XW], True, True), "m_p%d%d" % (u, b))
+            for e in events_x:
+                wait(pe, *e)
+            for b in (2 * h, 2 * h + 1):
+                if u:
+                    wait(pe, "ad%d%d0" % (u - 1, b))
+                    wait(pe, "ad%d%d1" % (u - 1, b))
+                inc(pe.matmul_mx(T["sb%d" % b][:, 0:TQ], kc[:, 128 * b:128 * b + 128], ks[:, 128 * b:128 * b + 128],
+                                 T.xc[:, 0:TQ], T.xs[:, 0:TQ], True, True), "m_s%d%d" % (u, b))
+
+    def copy_p(queue, u, b, banks):
+        bank, window = T[BANKS[b % banks]][:, 0:RT], T["pw%d" % u][:, RT * b:RT * b + RT]
+        wait(queue, "m_p%d%d" % (u, b))
+        if queue is v:
+            ins = v.tensor_copy(window, bank)
+        else:
+            ins = sc.activation(window, bank, ActivationFunctionType.Copy)
+        inc(ins, "c_p%d%d" % (u, b))
+
+    def pick(u, b, h):
+        off, at = T["off%d" % u], 24 * b + 12 * h
+        wait(sc, "c_p%d%d" % (u, b))
+        inc(sc.activation(T["pk%d" % u][:, TQ * b + HALF * h:TQ * b + HALF * h + HALF],
+                          T["pw%d" % u][:, RT * b:RT * b + RT].indirect(off[:, at:at + 12]), ActivationFunctionType.Copy), "ga%d%d%d" % (u, b, h))
+
+    def picks(u, banks):
+        copy_p(sc, u, 0, banks)
+        wait(sc, "o_o%d" % u)
+        for b, h in ((0, 0), (1, 0), (0, 1), (1, 1)):
+            pick(u, b, h)
+        copy_p(sc, u, 3, banks)
+        for b, h in ((2, 0), (3, 0), (2, 1), (3, 1)):
+            pick(u, b, h)
+
+    def add(u, b, h):
+        wait(v, "m_s%d%d" % (u, b))
+        wait(v, "ga%d%d%d" % (u, b, h))
+        inc(v.tensor_tensor(T["at%d" % u][:, 4 * HALF * h + b:4 * HALF * (h + 1):4], T["sb%d" % b][:, HALF * h:HALF * h + HALF],
+                            T["pk%d" % u][:, TQ * b + HALF * h:TQ * b + HALF * h + HALF], AluOpType.add), "ad%d%d%d" % (u, b, h))
+
+    def relu(u, b, hs, sem):
+        col = T["at%d" % u][:, 4 * HALF * hs[0] + b:4 * HALF * (hs[-1] + 1):4]
+        for h in hs:
+            wait(v, "ad%d%d%d" % (u, b, h))
+        inc(v.tensor_scalar(col, col, 0.0, 0.03125, AluOpType.max, AluOpType.mult), sem)
+
+    def elementwise(u, banks):
+        copy_p(v, u, 1, banks)
+        add(u, 0, 0)
+        add(u, 1, 0)
+        copy_p(v, u, 2, banks)
+        add(u, 0, 1)
+        add(u, 1, 1)
+        relu(u, 0, (0, 1), "rb%d" % u)
+        relu(u, 1, (0, 1), "rb%d" % u)
+        for h in range(2):
+            for b in (2, 3):
+                add(u, b, h)
+                relu(u, b, (h,), "rl%d%d" % (u, h))
+            if h == 0:
+                wait(v, "rb%d" % u, 2)
+            wait(v, "rl%d%d" % (u, h), 2)
+            a, e = HALF * h, HALF * h + HALF
+            inc(v.quantize_mx(T["ac%d" % u][:, a:e], T["as%d" % u][:, a:e], T["at%d" % u][:, 4 * a:4 * e]), "qa%d%d" % (u, h))
+
+    if core in posts:
+        c = users[posts.index(core)]
+        wait(g, "r_kpf", len(every))
+        send(move([c], [T.kpr[:]], T.kpf[:], "r_kp", out))
+    if core in relays:
+        b = relays.index(core)
+        wait(g, "r_kw", len(stay) if b < 2 else few)
+        send(move(users, [by(T.kc[:, 128 * b:128 * b + 128])] * 4, by(T.kw[:]), "r_k%d" % b, out))
+    per = len(out) // 4
+    for c, name, own, there, f in ((far[2], "r_vc", T.vo, T.vr, by), (far[3], "r_vs", T.vos, T.vrs, lambda t: t)):
+        if core == c:
+            wait(g, name, len(stay))
+            send(*[move([cores[(r + d) % N]], [f(there[:, 128 * (d - 1):128 * d])], f(own[:]), "r_v%d" % d, out[per * (d - 1):per * d])
+                   for d in (1, 2, 3, 4)])
+    if core in far:
+        wait(g, "sent", sent[0])
+        return
+
+    keys = [[("r_ks", len(out)), ("r_k%d" % b, len(out))] for b in range(4)]
+
+    if core in near:
+        d = near.index(core) + 1
+        offsets(0, T.kpr, ("r_kp", len(out)), ("r_q", len(stay)))
+        products(0, T.kc, T.kcs, 4, [keys[0] + [("r_x", 2 * len(every))]] + keys[1:], [])
+        picks(0, 4)
+        elementwise(0, 4)
+        a = TQ * (d - 1)
+        for h in range(2):
+            wait(g, "qa0%d" % h)
+            i, e = HALF * h, HALF * h + HALF
+            send(move([me], [by(T.ar[:, a + i:a + e])], by(T.ac0[:, i:e]), "r_a%d%d" % (d, h), every))
+            send(move([me], [T.ars[:, a + i:a + e]], T.as0[:, i:e], "r_a%d%d" % (d, h), every))
+        wait(g, "sent", sent[0])
+        return
+
+    inc(sy.dma_start(T.kpo[:], T.kp[:]), "l_kp", 16)
+    inc(sy.dma_start(T.kyb[:, 0:1024], T.ky[:, 0:1024]), "l_k0", 16)
+    inc(sy.dma_start(T.kyb[:, 1024:2048], T.ky[:, 1024:2048]), "l_k1", 16)
+    inc(sy.dma_start(T.rtb[:], T.rt[:]), "l_rt", 16)
+    for q in range(8):
+        inc(sc.dma_start(T.qr[16 * q:16 * q + 16, :], T.qp[:]), "l_qp", 16)
+    inc(sc.dma_start(T.qxb[:], T.qx[:]), "l_qx", 16)
+    inc(sc.dma_start(T.vvb[:], T.vv[:]), "l_vv", 16)
+
+    wait(g, "l_kp", 16)
+    send(move(posts, [T.kpf[:]] * 4, T.kpo[:], "r_kpf", every))
+
+    def piece(b, es):
+        return move([relays[b]], [by(T.kw[:])], by(T.ko[:, 128 * b:128 * b + 128]), "r_kw", es)
+
+    wait(g, "q_k0")
+    send(piece(0, out), piece(1, stay))
+    wait(g, "q_k1")
+    send(piece(2, stay[:few]), piece(3, stay[few:]), move(users, [T.kcs[:]] * 4, T.kos[:], "r_ks", out))
+    wait(g, "l_qp", 128)
+    send(move(near, [T.qr[:]] * 3, T.qr[:], "r_q", stay))
+    wait(g, "q_rt")
+    wait(g, "q_qx")
+    for a in (by(T.xc[:]), T.xs[:]):
+        send(move(near[::-1], [a] * 3, a, "r_x", every))
+    wait(g, "q_vv")
+    send(move([far[2]], [by(T.vo[:])], by(T.vo[:]), "r_vc", stay))
+    send(move([far[3]], [T.vos[:]], T.vos[:], "r_vs", out))
+    wait(g, "sent", sent[0])
+
+    for name, codes, plane, tile in (("k0", T.ko[:, 0:256], T.kos[:, 0:256], T.kyb[:, 0:1024]),
+                                     ("k1", T.ko[:, 256:512], T.kos[:, 256:512], T.kyb[:, 1024:2048]),
+                                     ("rt", T.xc[:, TQ:XW], T.xs[:, TQ:XW], T.rtb[:]),
+                                     ("qx", T.xc[:, 0:TQ], T.xs[:, 0:TQ], T.qxb[:])):
+        wait(v, "l_" + name, 16)
+        inc(v.quantize_mx(codes, plane, tile), "q_" + name)
+    offsets(0, T.kpo, ("l_kp", 16), ("l_qp", 128))
+    wait(v, "l_vv", 16)
+    inc(v.quantize_mx(T.vo[:], T.vos[:], T.vvb[:]), "q_vv")
+    elementwise(0, 4)
+    offsets(1, T.kpr, ("r_kp", len(out)), ("l_qp", 128))
+    elementwise(1, 2)
+
+    picks(0, 4)
+    picks(1, 2)
+
+    def value(vc, vs, ac, as_, a, h, start, stop):
+        i, e = a + HALF * h, a + HALF * h + HALF
+        ins = pe.matmul_mx(T["yb%d" % h][:, 0:HALF], vc, vs, ac[:, i:e], as_[:, i:e], start, stop)
+        if stop:
+            inc(ins, "m_y%d" % h)
+
+    def slot(d):
+        return T.vr[:, 128 * (d - 1):128 * d], T.vrs[:, 128 * (d - 1):128 * d]
+
+    products(0, T.ko, T.kos, 4, [[("q_k0", 1), ("q_rt", 1)], [], [("q_k1", 1)], []], [("q_qx", 1)])
+    for e in ("qa00", "qa01", "q_vv", "c_p02", "c_p03"):
+        wait(pe, e)
+    for h in range(2):
+        value(T.vo[:], T.vos[:], T.ac0, T.as0, 0, h, True, False)
+    products(1, T.kc, T.kcs, 2, keys, [])
+    for h in range(2):
+        for d in (4, 3, 1, 2):
+            wait(pe, "r_v%d" % d, 2 * per)
+            if d == 4:
+                wait(pe, "qa1%d" % h)
+                value(*slot(d), T.ac1, T.as1, 0, h, False, False)
+            else:
+                wait(pe, "r_a%d%d" % (d, h), 2 * len(every))
+                value(*slot(d), T.ar, T.ars, TQ * (d - 1), h, False, d == 2)
+
+    wait(sc, "m_y0")
+    inc(sc.activation(T.ysb[:, 0:HALF], T.yb0[:, 0:HALF], ActivationFunctionType.Copy), "c_y0")
+    wait(sc, "c_y0")
+    inc(sc.dma_start(T.y[:, 0:HALF], T.ysb[:, 0:HALF]), "st0", 16)
+    wait(v, "m_y1")
+    inc(v.tensor_copy(T.ysb[:, HALF:TQ], T.yb1[:, 0:HALF]), "c_y1")
+    wait(sy, "c_y1")
+    inc(sy.dma_start(T.y[:, HALF:TQ], T.ysb[:, HALF:TQ]), "st1", 16)
+    wait(sc, "st0", 16)
+    wait(sy, "st1", 16)

@@ -4,40 +4,38 @@ from concourse.mybir import dt, AluOpType, ActivationFunctionType
 N = 5
 TQ = 384
 RT = 256
-XW = TQ + RT
 HALF = TQ // 2
+K0, R0, Q0, V0, W = 0, 512, 512 + RT, 512 + RT + TQ, 512 + RT + TQ + 128
 
 SCRATCH = {
     "kyb": ("sbuf", [128, 2048], "bfloat16"),
     "qxb": ("sbuf", [128, 4 * TQ], "bfloat16"),
     "rtb": ("sbuf", [128, 4 * RT], "bfloat16"),
     "vvb": ("sbuf", [128, 512], "bfloat16"),
-    "ko": ("sbuf", [128, 512], "float8_e4m3fn_x4"),
-    "kos": ("sbuf", [128, 512], "uint8"),
-    "kw": ("sbuf", [128, 128], "float8_e4m3fn_x4"),
-    "kc": ("sbuf", [128, 512], "float8_e4m3fn_x4"),
-    "kcs": ("sbuf", [128, 512], "uint8"),
-    "xc": ("sbuf", [128, XW], "float8_e4m3fn_x4"),
-    "xs": ("sbuf", [128, XW], "uint8"),
-    "vo": ("sbuf", [128, 128], "float8_e4m3fn_x4"),
-    "vos": ("sbuf", [128, 128], "uint8"),
-    "vr": ("sbuf", [128, 512], "float8_e4m3fn_x4"),
-    "vrs": ("sbuf", [128, 512], "uint8"),
-    "ar": ("sbuf", [128, 3 * TQ], "float8_e4m3fn_x4"),
-    "ars": ("sbuf", [128, 3 * TQ], "uint8"),
+    "co": ("sbuf", [128, W], "float8_e4m3fn_x4"),
+    "so": ("sbuf", [128, W], "uint8"),
+    "ch": ("sbuf", [128, W], "float8_e4m3fn_x4"),
+    "sh": ("sbuf", [128, W], "uint8"),
+    "ck": ("sbuf", [128, 512], "float8_e4m3fn_x4"),
+    "sk": ("sbuf", [128, 512], "uint8"),
+    "cv": ("sbuf", [128, 512], "float8_e4m3fn_x4"),
+    "sv": ("sbuf", [128, 512], "uint8"),
+    "ca": ("sbuf", [128, 3 * TQ], "float8_e4m3fn_x4"),
+    "sa": ("sbuf", [128, 3 * TQ], "uint8"),
+    "pd": ("dram", [224, 4], "int32"),
+    "kh": ("dram", [128, 4], "int32"),
+    "qh": ("dram", [128, 4], "int32"),
     "kpo": ("sbuf", [128, 4], "int32"),
-    "kpf": ("sbuf", [128, 4], "int32"),
     "kpr": ("sbuf", [128, 4], "int32"),
     "qr": ("sbuf", [128, 24], "int32"),
     "ysb": ("sbuf", [128, TQ], "float32"),
 }
-BANKS = ["pb0", "pb1", "yb0", "yb1", "sb0", "sb1", "sb2", "sb3"]
+BANKS = ["b%d" % _i for _i in range(8)]
 for _n in BANKS:
     SCRATCH[_n] = ("psum", [128, 512], "float32")
 for _u in range(2):
     SCRATCH["kf%d" % _u] = ("sbuf", [128, 4], "float32")
     SCRATCH["ot%d" % _u] = ("sbuf", [128, 96], "float32")
-    SCRATCH["om%d" % _u] = ("sbuf", [128, 96], "float32")
     SCRATCH["off%d" % _u] = ("sbuf", [128, 96], "uint16")
     SCRATCH["pw%d" % _u] = ("sbuf", [128, 4 * RT], "float32")
     SCRATCH["pk%d" % _u] = ("sbuf", [128, 4 * TQ], "float32")
@@ -45,16 +43,32 @@ for _u in range(2):
     SCRATCH["ac%d" % _u] = ("sbuf", [128, TQ], "float8_e4m3fn_x4")
     SCRATCH["as%d" % _u] = ("sbuf", [128, TQ], "uint8")
 
-SEMAPHORES = ["l_k0", "l_k1", "l_rt", "l_qx", "l_vv", "l_kp", "l_qp",
-              "q_k0", "q_k1", "q_rt", "q_qx", "q_vv",
-              "r_kpf", "r_kp", "r_kw", "r_k0", "r_k1", "r_k2", "r_k3", "r_ks", "r_x", "r_q",
-              "r_vc", "r_vs", "r_v1", "r_v2", "r_v3", "r_v4", "r_a10", "r_a11", "r_a20", "r_a21", "r_a30", "r_a31",
+PARTS = {"a": (0, HALF), "z": (HALF, TQ), "w": (0, TQ)}
+VECTOR = [("cp", 1), ("cp", 2), ("ad", 0, "w"), ("ad", 1, "w"), ("rl", 0, "w"), ("ad", 2, "a"), ("rl", 1, "a"), ("ad", 3, "a"),
+          ("rl", 2, "a"), ("rl", 3, "a"), ("qa", 0, "a"), ("ad", 2, "z"), ("ad", 3, "z"), ("rl", 3, "z"), ("qa", 0, "z")]
+SCALAR = [("cp", 0), ("pk", 0, "w"), ("pk", 1, "w"), ("cp", 3), ("pk", 2, "a"), ("pk", 3, "a"), ("pk", 2, "z"), ("pk", 3, "z"),
+          ("rl", 1, "z"), ("rl", 2, "z")]
+TENSOR = [("mp", 0), ("mp", 1), ("mp", 2), ("ms", 0), ("ms", 1), ("mp", 3), ("ms", 2), ("ms", 3)]
+ARRIVAL = (2, 3, 0, 1)
+
+ROUTES = [(0, "G0", (1, 2, 3, 4)), (1, "H1", (1, 2, 3, 4)), (2, "G1", (1, 2, 3, 4)), (3, "H0", (1, 2, 3, 4)),
+          (4, "H2", (1, 2, 3, 4))]
+CALLS = [[(4, 0, 8), (0, 8, 12), (1, 12, 16)], [(2, 0, 8), (3, 8, 16)]]
+POSTS = ["H2", "G1", "H0", "G0"]
+RT_BY = "H0"
+QP_BY = None
+V_BY = [("G0", True, (1, 2, 3, 4)), ("G1", False, (1, 2, 3, 4))]
+V_LOAD = ("q_qx", 1)
+V_PACK = 99
+
+SEMAPHORES = ["l_ky", "l_rt", "l_qx", "l_vv", "l_kp", "l_qp", "l_pos", "q_ky", "q_rt", "q_qx", "q_vv",
+              "h_kp", "h_qp", "h_vc", "h_vs", "r_kp", "r_qp", "r_xs", "r_rt", "r_qx", "r_v1", "r_v2", "r_v3", "r_v4",
               "sent", "m_y0", "m_y1", "c_y0", "c_y1", "st0", "st1"]
+SEMAPHORES += ["%s%d" % (_n, _p) for _n in ("h_k", "r_k") for _p in range(5)]
+SEMAPHORES += ["r_a%d%s" % (_d, _s[2]) for _d in (1, 2, 3) for _s in VECTOR if _s[0] == "qa"]
 for _u in range(2):
-    SEMAPHORES += ["%s%d" % (_n, _u) for _n in ("o_k", "o_t", "o_m", "o_o", "rb")]
-    SEMAPHORES += ["%s%d%d" % (_n, _u, _h) for _n in ("rl", "qa") for _h in range(2)]
-    SEMAPHORES += ["%s%d%d" % (_n, _u, _b) for _n in ("m_p", "m_s", "c_p") for _b in range(4)]
-    SEMAPHORES += ["%s%d%d%d" % (_n, _u, _b, _h) for _n in ("ga", "ad") for _b in range(4) for _h in range(2)]
+    SEMAPHORES += ["%s%d" % (_n, _u) for _n in ("o_k", "o_t", "o_o")]
+    SEMAPHORES += ["%s%d%d%s" % (_s[0], _u, _s[1], "".join(_s[2:])) for _s in VECTOR + SCALAR + TENSOR]
 
 
 def bits(es):
@@ -62,260 +76,264 @@ def bits(es):
 
 
 def team(rank_core, topo):
-    mine = topo.cores_of(rank_core)
-    near = [c for c in mine if c != rank_core and topo.die(c) == topo.die(rank_core)]
-    far = [c for c in mine if topo.die(c) != topo.die(rank_core)]
-    return near[:3], far
+    names = {"R": rank_core}
+    others = [c for c in topo.cores_of(rank_core) if c != rank_core]
+    for letter, group in (("H", [c for c in others if topo.die(c) == topo.die(rank_core)]),
+                          ("G", [c for c in others if topo.die(c) != topo.die(rank_core)])):
+        for i, c in enumerate(group):
+            names["%s%d" % (letter, i)] = c
+    return names
+
+
+def meet(p, q):
+    return PARTS[p][0] < PARTS[q][1] and PARTS[q][0] < PARTS[p][1]
 
 
 def rank_program(g, core, T, topo):
     v, sc, pe, sy = g.vector, g.scalar, g.tensor, g.sync
     cores = list(T.cores)
     teams = [team(c, topo) for c in cores]
-    r = None
-    for i, c in enumerate(cores):
-        if core == c or core in teams[i][0] or core in teams[i][1]:
-            r = i
-    if r is None:
+    found = [(i, name) for i, t in enumerate(teams) for name, c in t.items() if c == core]
+    if not found:
         return
-    me = cores[r]
-    near, far = teams[r]
-    relays = [far[0], near[0], far[1], near[1]]
-    posts = [far[0], near[0], near[2], near[1]]
+    r, role = found[0]
+    me, mine = cores[r], teams[r]
+    near = [mine["H%d" % i] for i in range(3)]
+    posts = [mine[x] for x in POSTS]
     out = topo.engines(me, cores[(r + 1) % N])
-    every = topo.engines(me, far[0])
+    every = topo.engines(me, near[0])
     stay = [e for e in every if e not in out]
     few = len(stay) // 2
+    lanes = {p: every[a:e] for call in CALLS for p, a, e in call}
+    packs = [s[2] for s in VECTOR if s[0] == "qa"]
     sent = [0]
+    waited = set()
 
-    def worker(s, d):
-        i = (s + d) % N
-        return teams[i][0][d - 1] if d < 4 else cores[i]
-
-    users = [worker(r, d) for d in (1, 2, 3, 4)]
+    def worker(d):
+        return teams[(r + d) % N]["H%d" % (d - 1) if d < 4 else "R"]
 
     def wait(queue, name, n=1):
-        queue.wait_ge(T.sem[name], n)
+        key = ([q is queue for q in (g, v, sc, pe, sy)].index(True), name, n)
+        if key not in waited:
+            waited.add(key)
+            queue.wait_ge(T.sem[name], n)
 
     def inc(ins, name, n=1):
         ins.then_inc(T.sem[name], n)
 
-    def move(dsts, outs, src, sem, es):
+    def move(dsts, there, src, sem, es):
         ids = []
         for c in dsts:
             a = topo.addr(c)
             ids.append(DstId(rid=a[0], pnc=a[1]))
         sent[0] += len(es)
-        return RemoteDMATransfer(dst_ids=ids, dma_engine_mask=bits(es), remote_sem=T.sem[sem], srcs=[src], dsts=list(outs))
+        return RemoteDMATransfer(dst_ids=ids, dma_engine_mask=bits(es), remote_sem=T.sem[sem], srcs=[src], dsts=[there] * len(dsts))
 
     def send(*moves):
         g.remote_dma_fused(list(moves), local_sem=T.sem["sent"])
 
-    def by(t):
-        return t.bitcast(dt.uint8)
+    def by(t, a, e):
+        return t[:, a:e].bitcast(dt.uint8)
 
-    def offsets(u, kp, kp_event, q_event):
-        kf, ot, om, off = T["kf%d" % u], T["ot%d" % u], T["om%d" % u], T["off%d" % u]
+    def piece(p, codes, plane):
+        return by(codes, 128 * p, 128 * p + 128) if p < 4 else plane[:, K0:R0]
+
+    def offsets(u, kp, kp_event, qp_event=("l_qp", 128)):
+        kf, ot, off = T["kf%d" % u], T["ot%d" % u], T["off%d" % u]
         wait(v, *kp_event)
         inc(v.tensor_copy(kf[:], kp[:]), "o_k%d" % u)
-        wait(v, *q_event)
+        wait(v, *qp_event)
         wait(v, "o_k%d" % u)
         for b in range(4):
             inc(v.tensor_scalar(ot[:, 24 * b:24 * b + 24], T.qr[:], kf[:, b:b + 1], -128.0, AluOpType.subtract, AluOpType.max), "o_t%d" % u)
         wait(v, "o_t%d" % u, 4)
-        inc(v.tensor_scalar(om[:], ot[:], 127.0, 128.0, AluOpType.min, AluOpType.add), "o_m%d" % u)
-        wait(v, "o_m%d" % u)
-        inc(v.tensor_copy(off[:], om[:]), "o_o%d" % u)
+        inc(v.tensor_scalar(off[:], ot[:], 127.0, 128.0, AluOpType.min, AluOpType.add), "o_o%d" % u)
 
-    def products(u, kc, ks, banks, events, events_x):
-        for h in range(2):
-            for b in (2 * h, 2 * h + 1):
-                for e in events[b]:
-                    wait(pe, *e)
-                if b >= banks:
-                    wait(pe, "c_p%d%d" % (u, b - banks))
-                elif u:
-                    wait(pe, "c_p%d%d" % (u - 1, b))
-                    wait(pe, "c_p%d%d" % (u - 1, b + 2))
-                inc(pe.matmul_mx(T[BANKS[b % banks]][:, 0:RT], kc[:, 128 * b:128 * b + 128], ks[:, 128 * b:128 * b + 128],
-                                 T.xc[:, TQ:XW], T.xs[:, TQ:XW], True, True), "m_p%d%d" % (u, b))
-            for e in events_x:
-                wait(pe, *e)
-            for b in (2 * h, 2 * h + 1):
-                if u:
-                    wait(pe, "ad%d%d0" % (u - 1, b))
-                    wait(pe, "ad%d%d1" % (u - 1, b))
-                inc(pe.matmul_mx(T["sb%d" % b][:, 0:TQ], kc[:, 128 * b:128 * b + 128], ks[:, 128 * b:128 * b + 128],
-                                 T.xc[:, 0:TQ], T.xs[:, 0:TQ], True, True), "m_s%d%d" % (u, b))
+    def made(step, u, i, part):
+        return ["%s%d%d%s" % (s[0], u, s[1], s[2]) for s in VECTOR + SCALAR if s[0] == step and i in (None, s[1]) and meet(s[2], part)]
 
-    def copy_p(queue, u, b, banks):
-        bank, window = T[BANKS[b % banks]][:, 0:RT], T["pw%d" % u][:, RT * b:RT * b + RT]
-        wait(queue, "m_p%d%d" % (u, b))
-        if queue is v:
-            ins = v.tensor_copy(window, bank)
-        else:
-            ins = sc.activation(window, bank, ActivationFunctionType.Copy)
-        inc(ins, "c_p%d%d" % (u, b))
+    def products(u, steps, kc, ks, order, pbanks, has_k, has_r, has_q, free):
+        for step, i in steps:
+            b = order[i]
+            if step == "mp":
+                bank, a, e, events, after = BANKS[i % pbanks], R0, Q0, has_r, ["cp%d%d" % (u, i)]
+            else:
+                bank, a, e, events, after = BANKS[4 + i], Q0, V0, has_q, made("ad", u, i, "w")
+            for event in has_k[b] + events + free.get(bank, []):
+                wait(pe, *event)
+            inc(pe.matmul_mx(T[bank][:, 0:e - a], kc[:, 128 * b:128 * b + 128], ks[:, 128 * b:128 * b + 128],
+                             T.co[:, a:e], T.so[:, a:e], True, True), "%s%d%d" % (step, u, i))
+            free[bank] = [(x, 1) for x in after]
 
-    def pick(u, b, h):
-        off, at = T["off%d" % u], 24 * b + 12 * h
-        wait(sc, "c_p%d%d" % (u, b))
-        inc(sc.activation(T["pk%d" % u][:, TQ * b + HALF * h:TQ * b + HALF * h + HALF],
-                          T["pw%d" % u][:, RT * b:RT * b + RT].indirect(off[:, at:at + 12]), ActivationFunctionType.Copy), "ga%d%d%d" % (u, b, h))
+    def elementwise(queue, steps, u, order, pbanks):
+        tile, pw, pk, off = T["at%d" % u], T["pw%d" % u], T["pk%d" % u], T["off%d" % u]
+        for step in steps:
+            kind, i = step[:2]
+            b = order[i]
+            name = "%s%d%d%s" % (kind, u, i, "".join(step[2:]))
+            window = pw[:, RT * b:RT * b + RT]
+            if kind == "cp":
+                wait(queue, "mp%d%d" % (u, i))
+                bank = T[BANKS[i % pbanks]][:, 0:RT]
+                inc(v.tensor_copy(window, bank) if queue is v else sc.activation(window, bank, ActivationFunctionType.Copy), name)
+                continue
+            a, e = PARTS[step[2]]
+            picked, col = pk[:, TQ * b + a:TQ * b + e], tile[:, 4 * a + b:4 * e:4]
+            if kind == "pk":
+                needs = ["cp%d%d" % (u, i), "o_o%d" % u]
+            elif kind == "ad":
+                needs = ["ms%d%d" % (u, i)] + made("pk", u, i, step[2])
+            elif kind == "rl":
+                needs = made("ad", u, i, step[2])
+            else:
+                needs = made("rl", u, None, step[2])
+            for x in needs:
+                wait(queue, x)
+            if kind == "pk":
+                ins = sc.activation(picked, window.indirect(off[:, 24 * b + a // 16:24 * b + e // 16]), ActivationFunctionType.Copy)
+            elif kind == "ad":
+                ins = v.tensor_tensor(col, T[BANKS[4 + i]][:, a:e], picked, AluOpType.add)
+            elif kind == "qa":
+                ins = v.quantize_mx(T["ac%d" % u][:, a:e], T["as%d" % u][:, a:e], tile[:, 4 * a:4 * e])
+            elif queue is v:
+                ins = v.tensor_scalar(col, col, 0.0, 0.03125, AluOpType.max, AluOpType.mult)
+            else:
+                ins = sc.activation(col, col, ActivationFunctionType.Relu, scale=0.03125)
+            inc(ins, name)
 
-    def picks(u, banks):
-        copy_p(sc, u, 0, banks)
-        wait(sc, "o_o%d" % u)
-        for b, h in ((0, 0), (1, 0), (0, 1), (1, 1)):
-            pick(u, b, h)
-        copy_p(sc, u, 3, banks)
-        for b, h in ((2, 0), (3, 0), (2, 1), (3, 1)):
-            pick(u, b, h)
-
-    def add(u, b, h):
-        wait(v, "m_s%d%d" % (u, b))
-        wait(v, "ga%d%d%d" % (u, b, h))
-        inc(v.tensor_tensor(T["at%d" % u][:, 4 * HALF * h + b:4 * HALF * (h + 1):4], T["sb%d" % b][:, HALF * h:HALF * h + HALF],
-                            T["pk%d" % u][:, TQ * b + HALF * h:TQ * b + HALF * h + HALF], AluOpType.add), "ad%d%d%d" % (u, b, h))
-
-    def relu(u, b, hs, sem):
-        col = T["at%d" % u][:, 4 * HALF * hs[0] + b:4 * HALF * (hs[-1] + 1):4]
-        for h in hs:
-            wait(v, "ad%d%d%d" % (u, b, h))
-        inc(v.tensor_scalar(col, col, 0.0, 0.03125, AluOpType.max, AluOpType.mult), sem)
-
-    def elementwise(u, banks):
-        copy_p(v, u, 1, banks)
-        add(u, 0, 0)
-        add(u, 1, 0)
-        copy_p(v, u, 2, banks)
-        add(u, 0, 1)
-        add(u, 1, 1)
-        relu(u, 0, (0, 1), "rb%d" % u)
-        relu(u, 1, (0, 1), "rb%d" % u)
-        for h in range(2):
-            for b in (2, 3):
-                add(u, b, h)
-                relu(u, b, (h,), "rl%d%d" % (u, h))
-            if h == 0:
-                wait(v, "rb%d" % u, 2)
-            wait(v, "rl%d%d" % (u, h), 2)
-            a, e = HALF * h, HALF * h + HALF
-            inc(v.quantize_mx(T["ac%d" % u][:, a:e], T["as%d" % u][:, a:e], T["at%d" % u][:, 4 * a:4 * e]), "qa%d%d" % (u, h))
-
-    if core in posts:
-        c = users[posts.index(core)]
-        wait(g, "r_kpf", len(every))
-        send(move([c], [T.kpr[:]], T.kpf[:], "r_kp", out))
-    if core in relays:
-        b = relays.index(core)
-        wait(g, "r_kw", len(stay) if b < 2 else few)
-        send(move(users, [by(T.kc[:, 128 * b:128 * b + 128])] * 4, by(T.kw[:]), "r_k%d" % b, out))
-    per = len(out) // 4
-    for c, name, own, there, f in ((far[2], "r_vc", T.vo, T.vr, by), (far[3], "r_vs", T.vos, T.vrs, lambda t: t)):
-        if core == c:
-            wait(g, name, len(stay))
-            send(*[move([cores[(r + d) % N]], [f(there[:, 128 * (d - 1):128 * d])], f(own[:]), "r_v%d" % d, out[per * (d - 1):per * d])
-                   for d in (1, 2, 3, 4)])
-    if core in far:
-        wait(g, "sent", sent[0])
+    if role in POSTS:
+        wait(g, "h_kp", few)
+        send(move([worker(POSTS.index(role) + 1)], T.kpr[:], T.kh[:], "r_kp", out))
+    for p, relay, ds in ROUTES:
+        if role == relay:
+            wait(g, "h_k%d" % p, len(lanes[p]))
+            send(move([worker(d) for d in ds], piece(p, T.ck, T.sk), piece(p, T.ch, T.sh), "r_k%d" % p, out))
+    if role == RT_BY:
+        wait(g, "r_rt", len(every))
+        send(move([c for c in near if c != core], by(T.co, R0, Q0), by(T.co, R0, Q0), "r_rt", stay))
+    if role == QP_BY:
+        for q in range(8):
+            queue = (sy, sc)[q % 2]
+            wait(queue, "h_qp", few)
+            inc(queue.dma_start(T.qr[16 * q:16 * q + 16, :], T.qh[32:128, :]), "l_qp", 16)
+        wait(g, "l_qp", 128)
+        send(move(near, T.qr[:], T.qr[:], "r_qp", every))
+    for relay, codes, ds in V_BY:
+        if role == relay:
+            wait(g, "h_vc" if codes else "h_vs", len(stay))
+            per = len(out) // len(ds)
+            send(*[move([cores[(r + d) % N]], by(T.cv, 128 * d - 128, 128 * d) if codes else T.sv[:, 128 * d - 128:128 * d],
+                        by(T.ch, V0, W) if codes else T.sh[:, V0:W], "r_v%d" % d, out[per * i:per * i + per]) for i, d in enumerate(ds)])
+    if role[0] == "G":
+        if sent[0]:
+            wait(g, "sent", sent[0])
         return
 
-    keys = [[("r_ks", len(out)), ("r_k%d" % b, len(out))] for b in range(4)]
+    arrived = [[("r_k4", len(out)), ("r_k%d" % b, len(out))] for b in range(4)]
 
-    if core in near:
+    if role[0] == "H":
         d = near.index(core) + 1
-        offsets(0, T.kpr, ("r_kp", len(out)), ("r_q", len(stay)))
-        products(0, T.kc, T.kcs, 4, [keys[0] + [("r_x", 2 * len(every))]] + keys[1:], [])
-        picks(0, 4)
-        elementwise(0, 4)
-        a = TQ * (d - 1)
-        for h in range(2):
-            wait(g, "qa0%d" % h)
-            i, e = HALF * h, HALF * h + HALF
-            send(move([me], [by(T.ar[:, a + i:a + e])], by(T.ac0[:, i:e]), "r_a%d%d" % (d, h), every))
-            send(move([me], [T.ars[:, a + i:a + e]], T.as0[:, i:e], "r_a%d%d" % (d, h), every))
+        for q in range(0 if QP_BY else 8):
+            queue = (sy, sc)[q % 2]
+            wait(queue, "h_qp", few)
+            inc(queue.dma_start(T.qr[16 * q:16 * q + 16, :], T.qh[32:128, :]), "l_qp", 16)
+        offsets(0, T.kpr, ("r_kp", len(out)), ("r_qp", len(every)) if QP_BY else ("l_qp", 128))
+        products(0, TENSOR, T.ck, T.sk, ARRIVAL, 4, arrived,
+                 [("r_xs", len(every)), ("r_rt", len(every if role == RT_BY else stay))], [("r_qx", len(every))], {})
+        elementwise(sc, SCALAR, 0, ARRIVAL, 4)
+        elementwise(v, VECTOR, 0, ARRIVAL, 4)
+        for part in packs:
+            wait(g, "qa00" + part)
+            (a, e), at = PARTS[part], TQ * (d - 1)
+            send(move([me], by(T.ca, at + a, at + e), by(T.ac0, a, e), "r_a%d%s" % (d, part), every))
+            send(move([me], T.sa[:, at + a:at + e], T.as0[:, a:e], "r_a%d%s" % (d, part), every))
         wait(g, "sent", sent[0])
         return
 
-    inc(sy.dma_start(T.kpo[:], T.kp[:]), "l_kp", 16)
-    inc(sy.dma_start(T.kyb[:, 0:1024], T.ky[:, 0:1024]), "l_k0", 16)
-    inc(sy.dma_start(T.kyb[:, 1024:2048], T.ky[:, 1024:2048]), "l_k1", 16)
-    inc(sy.dma_start(T.rtb[:], T.rt[:]), "l_rt", 16)
+    inc(sy.dma_start(T.pd[0:128, :], T.kp[:]), "l_pos", 16)
+    inc(sc.dma_start(T.pd[128:224, :], T.qp[:]), "l_pos", 16)
+    inc(sy.dma_start(T.kyb[:], T.ky[:]), "l_ky", 16)
+    wait(sc, "l_pos", 32)
+    inc(sc.dma_start(T.rtb[:], T.rt[:]), "l_rt", 16)
+    inc(sc.dma_start(T.kpo[:], T.kp[:]), "l_kp", 16)
     for q in range(8):
         inc(sc.dma_start(T.qr[16 * q:16 * q + 16, :], T.qp[:]), "l_qp", 16)
-    inc(sc.dma_start(T.qxb[:], T.qx[:]), "l_qx", 16)
-    inc(sc.dma_start(T.vvb[:], T.vv[:]), "l_vv", 16)
+    inc(sy.dma_start(T.qxb[:], T.qx[:]), "l_qx", 16)
+    wait(sy, *V_LOAD)
+    inc(sy.dma_start(T.vvb[:], T.vv[:]), "l_vv", 16)
 
-    wait(g, "l_kp", 16)
-    send(move(posts, [T.kpf[:]] * 4, T.kpo[:], "r_kpf", every))
-
-    def piece(b, es):
-        return move([relays[b]], [by(T.kw[:])], by(T.ko[:, 128 * b:128 * b + 128]), "r_kw", es)
-
-    wait(g, "q_k0")
-    send(piece(0, out), piece(1, stay))
-    wait(g, "q_k1")
-    send(piece(2, stay[:few]), piece(3, stay[few:]), move(users, [T.kcs[:]] * 4, T.kos[:], "r_ks", out))
-    wait(g, "l_qp", 128)
-    send(move(near, [T.qr[:]] * 3, T.qr[:], "r_q", stay))
+    wait(g, "l_pos", 32)
+    send(move(posts, T.kh[:], T.pd[0:128, :], "h_kp", out[:few]),
+         move([mine[QP_BY]] if QP_BY else near, T.qh[:], T.pd[96:224, :], "h_qp", out[few:]))
+    wait(g, "q_ky")
+    for call in CALLS:
+        send(*[move([mine[x[1]] for x in ROUTES if x[0] == p], piece(p, T.ch, T.sh), piece(p, T.co, T.so), "h_k%d" % p, lanes[p])
+               for p, a, e in call])
     wait(g, "q_rt")
+    send(move([mine[RT_BY]], by(T.co, R0, Q0), by(T.co, R0, Q0), "r_rt", every))
     wait(g, "q_qx")
-    for a in (by(T.xc[:]), T.xs[:]):
-        send(move(near[::-1], [a] * 3, a, "r_x", every))
+    send(move(near, T.so[:, R0:V0], T.so[:, R0:V0], "r_xs", every))
+    send(move(near, by(T.co, Q0, V0), by(T.co, Q0, V0), "r_qx", every))
     wait(g, "q_vv")
-    send(move([far[2]], [by(T.vo[:])], by(T.vo[:]), "r_vc", stay))
-    send(move([far[3]], [T.vos[:]], T.vos[:], "r_vs", out))
+    send(move([mine[x[0]] for x in V_BY if x[1]], by(T.ch, V0, W), by(T.co, V0, W), "h_vc", stay))
+    send(move([mine[x[0]] for x in V_BY if not x[1]], T.sh[:, V0:W], T.so[:, V0:W], "h_vs", out))
     wait(g, "sent", sent[0])
 
-    for name, codes, plane, tile in (("k0", T.ko[:, 0:256], T.kos[:, 0:256], T.kyb[:, 0:1024]),
-                                     ("k1", T.ko[:, 256:512], T.kos[:, 256:512], T.kyb[:, 1024:2048]),
-                                     ("rt", T.xc[:, TQ:XW], T.xs[:, TQ:XW], T.rtb[:]),
-                                     ("qx", T.xc[:, 0:TQ], T.xs[:, 0:TQ], T.qxb[:])):
+    def pack(name, a, e, tile):
         wait(v, "l_" + name, 16)
-        inc(v.quantize_mx(codes, plane, tile), "q_" + name)
-    offsets(0, T.kpo, ("l_kp", 16), ("l_qp", 128))
-    wait(v, "l_vv", 16)
-    inc(v.quantize_mx(T.vo[:], T.vos[:], T.vvb[:]), "q_vv")
-    elementwise(0, 4)
-    offsets(1, T.kpr, ("r_kp", len(out)), ("l_qp", 128))
-    elementwise(1, 2)
+        inc(v.quantize_mx(T.co[:, a:e], T.so[:, a:e], tile), "q_" + name)
 
-    picks(0, 4)
-    picks(1, 2)
+    own = (0, 1, 2, 3)
 
-    def value(vc, vs, ac, as_, a, h, start, stop):
-        i, e = a + HALF * h, a + HALF * h + HALF
-        ins = pe.matmul_mx(T["yb%d" % h][:, 0:HALF], vc, vs, ac[:, i:e], as_[:, i:e], start, stop)
-        if stop:
+    pack("ky", K0, R0, T.kyb[:])
+    pack("rt", R0, Q0, T.rtb[:])
+    offsets(0, T.kpo, ("l_kp", 16))
+    elementwise(v, VECTOR[:2], 0, own, 4)
+    pack("qx", Q0, V0, T.qxb[:])
+    elementwise(v, VECTOR[2:V_PACK], 0, own, 4)
+    pack("vv", V0, W, T.vvb[:])
+    elementwise(v, VECTOR[V_PACK:], 0, own, 4)
+    offsets(1, T.kpr, ("r_kp", len(out)))
+    elementwise(v, VECTOR, 1, ARRIVAL, 2)
+
+    elementwise(sc, SCALAR, 0, own, 4)
+    elementwise(sc, SCALAR, 1, ARRIVAL, 2)
+
+    free = {}
+
+    def value(d, h):
+        part = "az"[h]
+        a, e = PARTS[part]
+        if d == 0:
+            vc, vs, events = T.co[:, V0:W], T.so[:, V0:W], [("q_vv", 1)] + free[BANKS[2 + h]]
+        else:
+            vc, vs, events = T.cv[:, 128 * d - 128:128 * d], T.sv[:, 128 * d - 128:128 * d], [("r_v%d" % d, sum(len(out) // len(x[2]) for x in V_BY if d in x[2]))]
+        if d % 4 == 0:
+            ac, as_, events = T["ac%d" % (d // 4)], T["as%d" % (d // 4)], events + [(x, 1) for x in made("qa", d // 4, None, part)]
+        else:
+            ac, as_, events = T.ca, T.sa, events + [("r_a%d%s" % (d, x), 2 * len(every)) for x in packs if meet(x, part)]
+            a, e = a + TQ * (d - 1), e + TQ * (d - 1)
+        for event in events:
+            wait(pe, *event)
+        ins = pe.matmul_mx(T[BANKS[2 + h]][:, 0:HALF], vc, vs, ac[:, a:e], as_[:, a:e], d == 0, d == 3)
+        if d == 3:
             inc(ins, "m_y%d" % h)
 
-    def slot(d):
-        return T.vr[:, 128 * (d - 1):128 * d], T.vrs[:, 128 * (d - 1):128 * d]
-
-    products(0, T.ko, T.kos, 4, [[("q_k0", 1), ("q_rt", 1)], [], [("q_k1", 1)], []], [("q_qx", 1)])
-    for e in ("qa00", "qa01", "q_vv", "c_p02", "c_p03"):
-        wait(pe, e)
-    for h in range(2):
-        value(T.vo[:], T.vos[:], T.ac0, T.as0, 0, h, True, False)
-    products(1, T.kc, T.kcs, 2, keys, [])
-    for h in range(2):
-        for d in (4, 3, 1, 2):
-            wait(pe, "r_v%d" % d, 2 * per)
-            if d == 4:
-                wait(pe, "qa1%d" % h)
-                value(*slot(d), T.ac1, T.as1, 0, h, False, False)
-            else:
-                wait(pe, "r_a%d%d" % (d, h), 2 * len(every))
-                value(*slot(d), T.ar, T.ars, TQ * (d - 1), h, False, d == 2)
+    products(0, sorted(TENSOR), T.co, T.so, own, 4, [[("q_ky", 1)]] * 4, [("q_rt", 1)], [("q_qx", 1)], free)
+    products(1, TENSOR, T.ck, T.sk, ARRIVAL, 2, arrived, [], [], free)
+    for d, h in VALUES:
+        value(d, h)
 
     wait(sc, "m_y0")
-    inc(sc.activation(T.ysb[:, 0:HALF], T.yb0[:, 0:HALF], ActivationFunctionType.Copy), "c_y0")
+    inc(sc.activation(T.ysb[:, 0:HALF], T[BANKS[2]][:, 0:HALF], ActivationFunctionType.Copy), "c_y0")
     wait(sc, "c_y0")
     inc(sc.dma_start(T.y[:, 0:HALF], T.ysb[:, 0:HALF]), "st0", 16)
     wait(v, "m_y1")
-    inc(v.tensor_copy(T.ysb[:, HALF:TQ], T.yb1[:, 0:HALF]), "c_y1")
+    inc(v.tensor_copy(T.ysb[:, HALF:TQ], T[BANKS[3]][:, 0:HALF]), "c_y1")
     wait(sy, "c_y1")
     inc(sy.dma_start(T.y[:, HALF:TQ], T.ysb[:, HALF:TQ]), "st1", 16)
     wait(sc, "st0", 16)
     wait(sy, "st1", 16)
+
+
+VALUES = [(0, 0), (0, 1)] + [(_d, _h) for _h in range(2) for _d in (4, 1, 2, 3)]

@@ -4,7 +4,7 @@ from concourse.mybir import dt, AluOpType, ActivationFunctionType
 N = 5
 TQ = 384
 RT = 256
-HALF = TQ // 2
+CUT = 256
 K0, R0, Q0, V0, W = 0, 512, 512 + RT, 512 + RT + TQ, 512 + RT + TQ + 128
 
 SCRATCH = {
@@ -14,19 +14,15 @@ SCRATCH = {
     "vvb": ("sbuf", [128, 512], "bfloat16"),
     "co": ("sbuf", [128, W], "float8_e4m3fn_x4"),
     "so": ("sbuf", [128, W], "uint8"),
-    "ch": ("sbuf", [128, W], "float8_e4m3fn_x4"),
-    "sh": ("sbuf", [128, W], "uint8"),
     "ck": ("sbuf", [128, 512], "float8_e4m3fn_x4"),
     "sk": ("sbuf", [128, 512], "uint8"),
     "cv": ("sbuf", [128, 512], "float8_e4m3fn_x4"),
     "sv": ("sbuf", [128, 512], "uint8"),
-    "ca": ("sbuf", [128, 3 * TQ], "float8_e4m3fn_x4"),
-    "sa": ("sbuf", [128, 3 * TQ], "uint8"),
+    "ca": ("sbuf", [128, 4 * TQ], "float8_e4m3fn_x4"),
+    "sa": ("sbuf", [128, 4 * TQ], "uint8"),
     "pd": ("dram", [224, 4], "int32"),
     "kh": ("dram", [128, 4], "int32"),
     "qh": ("dram", [128, 4], "int32"),
-    "kpo": ("sbuf", [128, 4], "int32"),
-    "kpr": ("sbuf", [128, 4], "int32"),
     "qr": ("sbuf", [128, 24], "int32"),
     "ysb": ("sbuf", [128, TQ], "float32"),
 }
@@ -34,8 +30,8 @@ BANKS = ["b%d" % _i for _i in range(8)]
 for _n in BANKS:
     SCRATCH[_n] = ("psum", [128, 512], "float32")
 for _u in range(2):
+    SCRATCH["kp%d" % _u] = ("sbuf", [128, 4], "int32")
     SCRATCH["kf%d" % _u] = ("sbuf", [128, 4], "float32")
-    SCRATCH["ot%d" % _u] = ("sbuf", [128, 96], "float32")
     SCRATCH["off%d" % _u] = ("sbuf", [128, 96], "uint16")
     SCRATCH["pw%d" % _u] = ("sbuf", [128, 4 * RT], "float32")
     SCRATCH["pk%d" % _u] = ("sbuf", [128, 4 * TQ], "float32")
@@ -43,32 +39,89 @@ for _u in range(2):
     SCRATCH["ac%d" % _u] = ("sbuf", [128, TQ], "float8_e4m3fn_x4")
     SCRATCH["as%d" % _u] = ("sbuf", [128, TQ], "uint8")
 
-PARTS = {"a": (0, HALF), "z": (HALF, TQ), "w": (0, TQ)}
-VECTOR = [("cp", 1), ("cp", 2), ("ad", 0, "w"), ("ad", 1, "w"), ("rl", 0, "w"), ("ad", 2, "a"), ("rl", 1, "a"), ("ad", 3, "a"),
-          ("rl", 2, "a"), ("rl", 3, "a"), ("qa", 0, "a"), ("ad", 2, "z"), ("ad", 3, "z"), ("rl", 3, "z"), ("qa", 0, "z")]
-SCALAR = [("cp", 0), ("pk", 0, "w"), ("pk", 1, "w"), ("cp", 3), ("pk", 2, "a"), ("pk", 3, "a"), ("pk", 2, "z"), ("pk", 3, "z"),
-          ("rl", 1, "z"), ("rl", 2, "z")]
-TENSOR = [("mp", 0), ("mp", 1), ("mp", 2), ("ms", 0), ("ms", 1), ("mp", 3), ("ms", 2), ("ms", 3)]
-ARRIVAL = (2, 3, 0, 1)
+PARTS = {"a": (0, CUT), "z": (CUT, TQ), "w": (0, TQ)}
+WHOLE = {
+    "v": [("cp", 1), ("cp", 2), ("ad", 0, "w"), ("ad", 1, "w"), ("rl", 0, "w"), ("ad", 2, "a"), ("rl", 1, "a"), ("ad", 3, "a"),
+          ("rl", 2, "a"), ("rl", 3, "a"), ("qa", 0, "a"), ("ad", 2, "z"), ("ad", 3, "z"), ("rl", 3, "z"), ("qa", 0, "z")],
+    "s": [("cp", 0), ("pk", 0, "w"), ("pk", 1, "w"), ("cp", 3), ("pk", 2, "a"), ("pk", 3, "a"), ("pk", 2, "z"), ("pk", 3, "z"),
+          ("rl", 1, "z"), ("rl", 2, "z")],
+    "p": [("mp", 0), ("mp", 1), ("mp", 2), ("ms", 0, "w"), ("ms", 1, "w"), ("mp", 3), ("ms", 2, "w"), ("ms", 3, "w")],
+}
 
-ROUTES = [(0, "G0", (1, 2, 3, 4)), (1, "H1", (1, 2, 3, 4)), (2, "G1", (1, 2, 3, 4)), (3, "H0", (1, 2, 3, 4)),
-          (4, "H2", (1, 2, 3, 4))]
-CALLS = [[(4, 0, 8), (0, 8, 12), (1, 12, 16)], [(2, 0, 8), (3, 8, 16)]]
-POSTS = ["H2", "G1", "H0", "G0"]
-RT_BY = "H0"
-QP_BY = None
-V_BY = [("G0", True, (1, 2, 3, 4)), ("G1", False, (1, 2, 3, 4))]
-V_LOAD = ("q_qx", 1)
-V_PACK = 99
+
+def one_part(x):
+    return {"v": [("cp", 1), ("cp", 3)] + [("ad", i, x) for i in range(4)] + [("rl", 2, x), ("rl", 3, x), ("qa", 0, x)],
+            "s": [("cp", 0), ("pk", 0, x), ("pk", 1, x), ("cp", 2), ("pk", 2, x), ("pk", 3, x), ("rl", 0, x), ("rl", 1, x)],
+            "p": [("mp", i) for i in range(4)] + [("ms", i, x) for i in range(4)]}
+
+
+MACHINE = 96
+WORKERS = ["H0", "H1", "H2", "R"]
+SHARE = "G3"
+ARRIVAL = (2, 3, 0, 1)
+SHARED = (2, 3, 0, 1)
+
+PIECES = {"k0": (True, 0, 128), "k1": (True, 128, 256), "k2": (True, 256, 384), "k3": (True, 384, 512), "ks": (False, K0, R0),
+          "rt": (True, R0, Q0), "xs": (False, R0, V0), "qx": (True, Q0, V0), "xa": (True, Q0, Q0 + CUT),
+          "r0": (True, R0, R0 + 128), "r1": (True, R0 + 128, Q0), "xz": (True, Q0 + CUT, V0), "rs": (False, R0, Q0), "qs": (False, Q0, V0), "vc": (True, V0, W), "vs": (False, V0, W)}
+ALL4 = (1, 2, 3, 4)
+SENDS = {
+    "R": [[("kp", ("H2", "G1", "H0", "G0", "G3"), 0, 8), ("qp", ("H0", "H1", "H2", "G3"), 8, 16)],
+          [("ks", ALL4, 0, 8)],
+          [("k2", ("G1",), 8, 12), ("k0", ("G0",), 12, 16)], [("k3", ("H0",), 8, 12), ("k1", ("H2",), 12, 16)],
+          [("rt", ("H0",), 8, 16)], [("xs", ("H0", "H1", "H2"), 8, 16)], [("qx", ("H0", "H1", "H2"), 0, 16)],
+          [("ks", ("G3",), 0, 16)],
+          [("vc", ("G0", "G1"), 0, 16)], [("vs", ("G2",), 0, 16)]],
+    "H0": [[("kp", (3,), 0, 8)], [("k3", ALL4, 0, 8)], [("rt", ("H1", "H2", "G3"), 8, 16)], [("k3", ("G3",), 8, 16)]],
+    "H1": [[("xs", ("G3",), 0, 16)], [("xa", ("G3",), 0, 16)]],
+    "H2": [[("kp", (1,), 0, 8)], [("k1", ALL4, 0, 8)], [("k1", ("G3",), 8, 16)]],
+    "G0": [[("kp", (4,), 0, 8)], [("k0", ALL4, 0, 8)], [("k0", ("G3",), 8, 16)], [("vc", (1,), 0, 4), ("vc", (2,), 4, 8)]],
+    "G1": [[("kp", (2,), 0, 8)], [("k2", ALL4, 0, 8)], [("k2", ("G3",), 8, 16)], [("vc", (3,), 0, 4), ("vc", (4,), 4, 8)]],
+    "G2": [[("vs", (d,), 2 * d - 2, 2 * d) for d in ALL4]],
+    "G3": [],
+}
+LOADS = [("y", "ky", None), ("y", "pos", None), ("s", "rt", ("l_pos", 32)), ("y", "qx", None), ("y", "vv", ("q_rt", 1))]
+R_VECTOR = ["ky", "of", "rt", "qx", 2, "vv"]
+VALUES = [(0, "z"), (0, "a"), (1, "a"), (2, "a"), (4, "a"), (3, "a"), (1, "z"), (2, "z"), (4, "z"), (3, "z")]
+
+H = ("H0", "H1", "H2")
+WHOLE = {"v": [("cp", 1), ("pk", 1, "w"), ("ad", 0, "w"), ("cp", 3), ("ad", 1, "w"), ("ad", 2, "w"), ("rl", 1, "a"), ("ad", 3, "a"), ("rl", 3, "a"),
+               ("qa", 0, "a"), ("ad", 3, "z"), ("rl", 3, "z"), ("qa", 0, "z")],
+         "s": [("cp", 0), ("pk", 0, "w"), ("cp", 2), ("pk", 2, "w"), ("pk", 3, "a"), ("rl", 0, "w"), ("rl", 2, "a"), ("pk", 3, "z"), ("rl", 2, "z"),
+               ("rl", 1, "z")],
+         "p": [("mp", 0), ("mp", 1), ("ms", 0, "w"), ("ms", 1, "w"), ("mp", 2), ("mp", 3), ("ms", 2, "w"), ("ms", 3, "w")]}
+SHARE = None
+A_LANES = [16, 16, 16, 16]
+V_TO = {"vc": "R", "vs": "R"}
+ARRIVAL = [(2, 3, 0, 1)] * 4
+LOADS = [("y", "ky", None), ("y", "rt", None), ("y", "pos", None), ("s", "qx", ("l_pos", 32)), ("s", "vv", None)]
+SENDS = {
+    "R": [[("kp", ("G1", "H0", "H2", "G0"), 0, 2)], [("qp", ("H0",), 8, 16), ("qp", ("H1",), 4, 8), ("qp", ("H2",), 2, 4)],
+          [("ks", ALL4, 0, 8), ("k2", ("G1",), 8, 12), ("k3", ("H0",), 12, 16)],
+          [("r0", ("H2",), 8, 12), ("r1", ("H0",), 12, 16)],
+          [("k0", ("G0",), 8, 12), ("k1", ("H2",), 12, 16)],
+          [("xs", H, 8, 16)], [("qx", ("H0", "H1"), 0, 8), ("qx", ("H2",), 8, 16)],
+          [("vc", ("G0", "G1"), 0, 16)], [("vs", ("G1", "H1"), 0, 16)]],
+    "H0": [[("kp", (3,), 0, 8)], [("k3", ALL4, 0, 8)], [("r1", ("H1", "H2"), 8, 16)]],
+    "H1": [[("vs", (1,), 0, 4), ("vs", (2,), 4, 8)]],
+    "H2": [[("kp", (1,), 0, 8)], [("r0", ("H0", "H1"), 8, 16)], [("k1", ALL4, 0, 8)]],
+    "G0": [[("kp", (4,), 0, 8)], [("k0", ALL4, 0, 8)], [("vc", (1,), 0, 4), ("vc", (2,), 4, 8)]],
+    "G1": [[("kp", (2,), 0, 8)], [("k2", ALL4, 0, 8)], [("vc", (3,), 0, 4), ("vc", (4,), 4, 8)], [("vs", (3,), 0, 4), ("vs", (4,), 4, 8)]],
+}
+R_VECTOR = ["ky", "rt", "of", "qx", 2, "vv"]
+VALUES = [(0, "a"), (0, "z"), (1, "a"), (1, "z"), (4, "a"), (2, "a"), (4, "z"), (3, "a"), (2, "z"), (3, "z")]
 
 SEMAPHORES = ["l_ky", "l_rt", "l_qx", "l_vv", "l_kp", "l_qp", "l_pos", "q_ky", "q_rt", "q_qx", "q_vv",
-              "h_kp", "h_qp", "h_vc", "h_vs", "r_kp", "r_qp", "r_xs", "r_rt", "r_qx", "r_v1", "r_v2", "r_v3", "r_v4",
-              "sent", "m_y0", "m_y1", "c_y0", "c_y1", "st0", "st1"]
-SEMAPHORES += ["%s%d" % (_n, _p) for _n in ("h_k", "r_k") for _p in range(5)]
-SEMAPHORES += ["r_a%d%s" % (_d, _s[2]) for _d in (1, 2, 3) for _s in VECTOR if _s[0] == "qa"]
-for _u in range(2):
-    SEMAPHORES += ["%s%d" % (_n, _u) for _n in ("o_k", "o_t", "o_o")]
-    SEMAPHORES += ["%s%d%d%s" % (_s[0], _u, _s[1], "".join(_s[2:])) for _s in VECTOR + SCALAR + TENSOR]
+              "sent", "m_ya", "m_yz", "c_ya", "c_yz", "sta", "stz", "kf0", "kf1", "of0", "of1"]
+SEMAPHORES += ["h_" + _p for _p in list(PIECES) + ["kp", "qp", "VC", "VS"]] + ["r_k" + _p for _p in "0123sp"]
+SEMAPHORES += ["r_%s%d" % (_p, _d) for _p in ("vc", "vs") for _d in ALL4] + ["r_a%d%s" % (_d, _x) for _d in range(4) for _x in "azw"]
+
+
+def label(u, step):
+    return "%s%d%d%s" % (step[0], u, step[1], "".join(step[2:]))
+
+
+SEMAPHORES += sorted({label(_u, _s) for _u, _plan in ((0, WHOLE), (1, WHOLE)) for _q in _plan.values() for _s in _q})
 
 
 def bits(es):
@@ -77,16 +130,17 @@ def bits(es):
 
 def team(rank_core, topo):
     names = {"R": rank_core}
-    others = [c for c in topo.cores_of(rank_core) if c != rank_core]
-    for letter, group in (("H", [c for c in others if topo.die(c) == topo.die(rank_core)]),
-                          ("G", [c for c in others if topo.die(c) != topo.die(rank_core)])):
-        for i, c in enumerate(group):
-            names["%s%d" % (letter, i)] = c
+    mate = [c for c in range(MACHINE) if topo.mates(topo.chip(c), topo.chip(rank_core)) and topo.may_write(c, rank_core)]
+    others = sorted((c for c in topo.cores_of(rank_core) if c != rank_core), key=lambda c: topo.may_write(c, mate[0]))
+    for letters, group in (("HG", others), ("MF", mate)):
+        for letter, same in zip(letters, (True, False)):
+            for i, c in enumerate([c for c in group if (topo.die(c) == topo.die(rank_core)) == same]):
+                names["%s%d" % (letter, i)] = c
     return names
 
 
 def meet(p, q):
-    return PARTS[p][0] < PARTS[q][1] and PARTS[q][0] < PARTS[p][1]
+    return p[0] < q[1] and q[0] < p[1]
 
 
 def rank_program(g, core, T, topo):
@@ -98,19 +152,10 @@ def rank_program(g, core, T, topo):
         return
     r, role = found[0]
     me, mine = cores[r], teams[r]
-    near = [mine["H%d" % i] for i in range(3)]
-    posts = [mine[x] for x in POSTS]
     out = topo.engines(me, cores[(r + 1) % N])
-    every = topo.engines(me, near[0])
-    stay = [e for e in every if e not in out]
-    few = len(stay) // 2
-    lanes = {p: every[a:e] for call in CALLS for p, a, e in call}
-    packs = [s[2] for s in VECTOR if s[0] == "qa"]
+    every = out + [e for e in topo.engines(me, mine["H0"]) if e not in out]
     sent = [0]
     waited = set()
-
-    def worker(d):
-        return teams[(r + d) % N]["H%d" % (d - 1) if d < 4 else "R"]
 
     def wait(queue, name, n=1):
         key = ([q is queue for q in (g, v, sc, pe, sy)].index(True), name, n)
@@ -132,208 +177,206 @@ def rank_program(g, core, T, topo):
     def send(*moves):
         g.remote_dma_fused(list(moves), local_sem=T.sem["sent"])
 
-    def by(t, a, e):
-        return t[:, a:e].bitcast(dt.uint8)
+    def run(codes, plane, is_codes, a, e):
+        return codes[:, a:e].bitcast(dt.uint8) if is_codes else plane[:, a:e]
 
-    def piece(p, codes, plane):
-        return by(codes, 128 * p, 128 * p + 128) if p < 4 else plane[:, K0:R0]
+    def name_of(p, to):
+        return to if to in mine else V_TO[p] if p[0] == "v" else WORKERS[to - 1]
 
-    def offsets(u, kp, kp_event, qp_event=("l_qp", 128)):
-        kf, ot, off = T["kf%d" % u], T["ot%d" % u], T["off%d" % u]
+    def sem_of(p, to):
+        return "h_" + p if to in mine else "r_%s%d" % (p, to) if p[0] == "v" else "r_" + p
+
+    landed = {sem_of(p, to): e - a for calls in SENDS.values() for c in calls for p, tos, a, e in c for to in tos if name_of(p, to) == role}
+
+    def here(is_codes, a, e):
+        if role == "R":
+            return [("q_" + n, 1) for n, span in (("ky", (K0, R0)), ("rt", (R0, Q0)), ("qx", (Q0, V0)), ("vv", (V0, W))) if meet(span, (a, e))]
+        return [("h_" + p, landed["h_" + p]) for p, x in PIECES.items() if "h_" + p in landed and x[0] == is_codes and meet(x[1:], (a, e))]
+
+    def transfer(p, tos, first, end):
+        far = tos[0] not in mine
+        dsts = [teams[(r + to) % N][name_of(p, to)] if far else mine[to] for to in tos]
+        if p in PIECES:
+            c, a, e = PIECES[p]
+            events, src = here(c, a, e), run(T.co, T.so, c, a, e)
+            there = src if not far else run(T.cv, T.sv, c, 128 * tos[0] - 128, 128 * tos[0]) if p[0] == "v" else run(T.ck, T.sk, c, a, e)
+        elif p in ("VC", "VS"):
+            events = [(x, landed[x]) for x in ["r_%s%d" % (p.lower(), d) for d in ALL4]]
+            src = there = run(T.cv, T.sv, p == "VC", 0, 512)
+        elif role == "R":
+            events, src, there = [("l_pos", 32)], T.pd[0:128, :] if p == "kp" else T.pd[96:224, :], T.kh[:] if p == "kp" else T.qh[:]
+        elif p == "kp":
+            events, src, there = [("h_kp", landed["h_kp"])], T.kh[:], T.kp1[:]
+        else:
+            events, src, there = [("h_qp", landed["h_qp"])], T.qh[:], T.qh[:]
+        for event in events:
+            wait(g, *event)
+        return move(dsts, there, src, sem_of(p, tos[0]), every[first:end])
+
+    for c in SENDS.get(role, []):
+        send(*[transfer(*x) for x in c])
+
+    def offsets(u, kp_event):
+        kf, off = T["kf%d" % u], T["off%d" % u]
         wait(v, *kp_event)
-        inc(v.tensor_copy(kf[:], kp[:]), "o_k%d" % u)
-        wait(v, *qp_event)
-        wait(v, "o_k%d" % u)
+        inc(v.tensor_scalar(kf[:], T["kp%d" % u][:], 128.0, None, AluOpType.subtract), "kf%d" % u)
+        wait(v, "l_qp", 128)
+        wait(v, "kf%d" % u)
         for b in range(4):
-            inc(v.tensor_scalar(ot[:, 24 * b:24 * b + 24], T.qr[:], kf[:, b:b + 1], -128.0, AluOpType.subtract, AluOpType.max), "o_t%d" % u)
-        wait(v, "o_t%d" % u, 4)
-        inc(v.tensor_scalar(off[:], ot[:], 127.0, 128.0, AluOpType.min, AluOpType.add), "o_o%d" % u)
+            inc(v.tensor_scalar(off[:, 24 * b:24 * b + 24], T.qr[:], kf[:, b:b + 1], RT - 1.0, AluOpType.subtract, AluOpType.min), "of%d" % u)
 
-    def made(step, u, i, part):
-        return ["%s%d%d%s" % (s[0], u, s[1], s[2]) for s in VECTOR + SCALAR if s[0] == step and i in (None, s[1]) and meet(s[2], part)]
+    def made(plan, u, kind, i, part):
+        return [label(u, s) for s in plan["v"] + plan["s"] + plan["p"] if s[0] == kind and i in (None, s[1]) and meet(PARTS[s[2]], PARTS[part])]
 
-    def products(u, steps, kc, ks, order, pbanks, has_k, has_r, has_q, free):
-        for step, i in steps:
+    free = {}
+
+    def products(u, plan, order, pbanks):
+        kc, ks = (T.ck, T.sk) if u else (T.co, T.so)
+        for step in plan["p"]:
+            i = step[1]
             b = order[i]
-            if step == "mp":
-                bank, a, e, events, after = BANKS[i % pbanks], R0, Q0, has_r, ["cp%d%d" % (u, i)]
+            if step[0] == "mp":
+                bank, a, e, after = BANKS[i % pbanks], R0, Q0, [label(u, ("cp", i))]
             else:
-                bank, a, e, events, after = BANKS[4 + i], Q0, V0, has_q, made("ad", u, i, "w")
-            for event in has_k[b] + events + free.get(bank, []):
+                bank, a, e, after = BANKS[4 + i], Q0 + PARTS[step[2]][0], Q0 + PARTS[step[2]][1], made(plan, u, "ad", i, "w")
+            keys = [(x, landed[x]) for x in ("r_ks", "r_k%d" % b)] if u else here(False, K0, R0) + here(True, 128 * b, 128 * b + 128)
+            for event in keys + here(False, a, e) + here(True, a, e) + free.get(bank, []):
                 wait(pe, *event)
             inc(pe.matmul_mx(T[bank][:, 0:e - a], kc[:, 128 * b:128 * b + 128], ks[:, 128 * b:128 * b + 128],
-                             T.co[:, a:e], T.so[:, a:e], True, True), "%s%d%d" % (step, u, i))
+                             T.co[:, a:e], T.so[:, a:e], True, True), label(u, step))
             free[bank] = [(x, 1) for x in after]
 
-    def elementwise(queue, steps, u, order, pbanks):
+    def elementwise(queue, steps, u, plan, order, pbanks):
         tile, pw, pk, off = T["at%d" % u], T["pw%d" % u], T["pk%d" % u], T["off%d" % u]
+        first = PARTS[plan["p"][-1][2]][0]
         for step in steps:
             kind, i = step[:2]
             b = order[i]
-            name = "%s%d%d%s" % (kind, u, i, "".join(step[2:]))
             window = pw[:, RT * b:RT * b + RT]
             if kind == "cp":
-                wait(queue, "mp%d%d" % (u, i))
+                wait(queue, label(u, ("mp", i)))
                 bank = T[BANKS[i % pbanks]][:, 0:RT]
-                inc(v.tensor_copy(window, bank) if queue is v else sc.activation(window, bank, ActivationFunctionType.Copy), name)
+                inc(v.tensor_copy(window, bank) if queue is v else sc.activation(window, bank, ActivationFunctionType.Copy), label(u, step))
                 continue
             a, e = PARTS[step[2]]
             picked, col = pk[:, TQ * b + a:TQ * b + e], tile[:, 4 * a + b:4 * e:4]
             if kind == "pk":
-                needs = ["cp%d%d" % (u, i), "o_o%d" % u]
+                wait(queue, "of%d" % u, 4)
+                needs = [label(u, ("cp", i))]
             elif kind == "ad":
-                needs = ["ms%d%d" % (u, i)] + made("pk", u, i, step[2])
+                needs = made(plan, u, "ms", i, step[2]) + made(plan, u, "pk", i, step[2])
             elif kind == "rl":
-                needs = made("ad", u, i, step[2])
+                needs = made(plan, u, "ad", i, step[2])
             else:
-                needs = made("rl", u, None, step[2])
+                needs = made(plan, u, "rl", None, step[2])
             for x in needs:
                 wait(queue, x)
             if kind == "pk":
-                ins = sc.activation(picked, window.indirect(off[:, 24 * b + a // 16:24 * b + e // 16]), ActivationFunctionType.Copy)
+                pick = window.indirect(off[:, 24 * b + a // 16:24 * b + e // 16])
+                ins = v.tensor_copy(picked, pick) if queue is v else sc.activation(picked, pick, ActivationFunctionType.Copy)
             elif kind == "ad":
-                ins = v.tensor_tensor(col, T[BANKS[4 + i]][:, a:e], picked, AluOpType.add)
+                ins = v.tensor_tensor(col, T[BANKS[4 + i]][:, a - first:e - first], picked, AluOpType.add)
             elif kind == "qa":
                 ins = v.quantize_mx(T["ac%d" % u][:, a:e], T["as%d" % u][:, a:e], tile[:, 4 * a:4 * e])
             elif queue is v:
                 ins = v.tensor_scalar(col, col, 0.0, 0.03125, AluOpType.max, AluOpType.mult)
             else:
                 ins = sc.activation(col, col, ActivationFunctionType.Relu, scale=0.03125)
-            inc(ins, name)
+            inc(ins, label(u, step))
 
-    if role in POSTS:
-        wait(g, "h_kp", few)
-        send(move([worker(POSTS.index(role) + 1)], T.kpr[:], T.kh[:], "r_kp", out))
-    for p, relay, ds in ROUTES:
-        if role == relay:
-            wait(g, "h_k%d" % p, len(lanes[p]))
-            send(move([worker(d) for d in ds], piece(p, T.ck, T.sk), piece(p, T.ch, T.sh), "r_k%d" % p, out))
-    if role == RT_BY:
-        wait(g, "r_rt", len(every))
-        send(move([c for c in near if c != core], by(T.co, R0, Q0), by(T.co, R0, Q0), "r_rt", stay))
-    if role == QP_BY:
+    def repeat(table, queues, event=None):
         for q in range(8):
-            queue = (sy, sc)[q % 2]
-            wait(queue, "h_qp", few)
-            inc(queue.dma_start(T.qr[16 * q:16 * q + 16, :], T.qh[32:128, :]), "l_qp", 16)
-        wait(g, "l_qp", 128)
-        send(move(near, T.qr[:], T.qr[:], "r_qp", every))
-    for relay, codes, ds in V_BY:
-        if role == relay:
-            wait(g, "h_vc" if codes else "h_vs", len(stay))
-            per = len(out) // len(ds)
-            send(*[move([cores[(r + d) % N]], by(T.cv, 128 * d - 128, 128 * d) if codes else T.sv[:, 128 * d - 128:128 * d],
-                        by(T.ch, V0, W) if codes else T.sh[:, V0:W], "r_v%d" % d, out[per * i:per * i + per]) for i, d in enumerate(ds)])
-    if role[0] == "G":
-        if sent[0]:
-            wait(g, "sent", sent[0])
-        return
+            queue = queues[q % len(queues)]
+            if event:
+                wait(queue, *event)
+            inc(queue.dma_start(T.qr[16 * q:16 * q + 16, :], table), "l_qp", 16)
 
-    arrived = [[("r_k4", len(out)), ("r_k%d" % b, len(out))] for b in range(4)]
-
-    if role[0] == "H":
-        d = near.index(core) + 1
-        for q in range(0 if QP_BY else 8):
-            queue = (sy, sc)[q % 2]
-            wait(queue, "h_qp", few)
-            inc(queue.dma_start(T.qr[16 * q:16 * q + 16, :], T.qh[32:128, :]), "l_qp", 16)
-        offsets(0, T.kpr, ("r_kp", len(out)), ("r_qp", len(every)) if QP_BY else ("l_qp", 128))
-        products(0, TENSOR, T.ck, T.sk, ARRIVAL, 4, arrived,
-                 [("r_xs", len(every)), ("r_rt", len(every if role == RT_BY else stay))], [("r_qx", len(every))], {})
-        elementwise(sc, SCALAR, 0, ARRIVAL, 4)
-        elementwise(v, VECTOR, 0, ARRIVAL, 4)
-        for part in packs:
-            wait(g, "qa00" + part)
-            (a, e), at = PARTS[part], TQ * (d - 1)
-            send(move([me], by(T.ca, at + a, at + e), by(T.ac0, a, e), "r_a%d%s" % (d, part), every))
-            send(move([me], T.sa[:, at + a:at + e], T.as0[:, a:e], "r_a%d%s" % (d, part), every))
+    if role in WORKERS[:3] or role == SHARE:
+        u, d, plan, order = (0, 0, one_part("a"), SHARED) if role == SHARE else (1, WORKERS.index(role) + 1, WHOLE, ARRIVAL[WORKERS.index(role)])
+        if role == SHARE:
+            wait(sy, "h_kp", landed["h_kp"])
+            inc(sy.dma_start(T.kp0[:], T.kh[:]), "l_kp", 16)
+        repeat(T.qh[32:128, :], (sy, sc), ("h_qp", landed["h_qp"]))
+        offsets(u, ("r_kp", landed["r_kp"]) if u else ("l_kp", 16))
+        products(u, plan, order, 4)
+        elementwise(sc, plan["s"], u, plan, order, 4)
+        elementwise(v, plan["v"], u, plan, order, 4)
+        for step in plan["v"]:
+            if step[0] == "qa":
+                wait(g, label(u, step))
+                a, e = PARTS[step[2]]
+                for c in (True, False):
+                    send(move([me], run(T.ca, T.sa, c, TQ * d + a, TQ * d + e), run(T["ac%d" % u], T["as%d" % u], c, a, e),
+                              "r_a%d%s" % (d, step[2]), every[:A_LANES[d]]))
+    if sent[0]:
         wait(g, "sent", sent[0])
+    if role != "R":
         return
 
     inc(sy.dma_start(T.pd[0:128, :], T.kp[:]), "l_pos", 16)
     inc(sc.dma_start(T.pd[128:224, :], T.qp[:]), "l_pos", 16)
-    inc(sy.dma_start(T.kyb[:], T.ky[:]), "l_ky", 16)
-    wait(sc, "l_pos", 32)
-    inc(sc.dma_start(T.rtb[:], T.rt[:]), "l_rt", 16)
-    inc(sc.dma_start(T.kpo[:], T.kp[:]), "l_kp", 16)
-    for q in range(8):
-        inc(sc.dma_start(T.qr[16 * q:16 * q + 16, :], T.qp[:]), "l_qp", 16)
-    inc(sy.dma_start(T.qxb[:], T.qx[:]), "l_qx", 16)
-    wait(sy, *V_LOAD)
-    inc(sy.dma_start(T.vvb[:], T.vv[:]), "l_vv", 16)
+    tiles = {"ky": (K0, R0, T.kyb, T.ky), "rt": (R0, Q0, T.rtb, T.rt), "qx": (Q0, V0, T.qxb, T.qx), "vv": (V0, W, T.vvb, T.vv)}
+    for key, what, event in LOADS:
+        queue = sy if key == "y" else sc
+        if event:
+            wait(queue, *event)
+        if what == "pos":
+            inc(queue.dma_start(T.kp0[:], T.kp[:]), "l_kp", 16)
+            repeat(T.qp[:], (queue,))
+        else:
+            inc(queue.dma_start(tiles[what][2][:], tiles[what][3][:]), "l_" + what, 16)
 
-    wait(g, "l_pos", 32)
-    send(move(posts, T.kh[:], T.pd[0:128, :], "h_kp", out[:few]),
-         move([mine[QP_BY]] if QP_BY else near, T.qh[:], T.pd[96:224, :], "h_qp", out[few:]))
-    wait(g, "q_ky")
-    for call in CALLS:
-        send(*[move([mine[x[1]] for x in ROUTES if x[0] == p], piece(p, T.ch, T.sh), piece(p, T.co, T.so), "h_k%d" % p, lanes[p])
-               for p, a, e in call])
-    wait(g, "q_rt")
-    send(move([mine[RT_BY]], by(T.co, R0, Q0), by(T.co, R0, Q0), "r_rt", every))
-    wait(g, "q_qx")
-    send(move(near, T.so[:, R0:V0], T.so[:, R0:V0], "r_xs", every))
-    send(move(near, by(T.co, Q0, V0), by(T.co, Q0, V0), "r_qx", every))
-    wait(g, "q_vv")
-    send(move([mine[x[0]] for x in V_BY if x[1]], by(T.ch, V0, W), by(T.co, V0, W), "h_vc", stay))
-    send(move([mine[x[0]] for x in V_BY if not x[1]], T.sh[:, V0:W], T.so[:, V0:W], "h_vs", out))
-    wait(g, "sent", sent[0])
+    own, plan = (0, 1, 2, 3), one_part("z") if SHARE else dict(WHOLE, p=sorted(WHOLE["p"]))
+    done = 0
+    for x in R_VECTOR:
+        if x == "of":
+            offsets(0, ("l_kp", 16))
+        elif x in tiles:
+            a, e, tile, _ = tiles[x]
+            wait(v, "l_" + x, 16)
+            inc(v.quantize_mx(T.co[:, a:e], T.so[:, a:e], tile[:]), "q_" + x)
+        else:
+            elementwise(v, plan["v"][done:x], 0, plan, own, 4)
+            done = x
+    elementwise(v, plan["v"][done:], 0, plan, own, 4)
+    offsets(1, ("r_kp", landed["r_kp"]))
+    elementwise(v, WHOLE["v"], 1, WHOLE, ARRIVAL[3], 2)
+    elementwise(sc, plan["s"], 0, plan, own, 4)
+    elementwise(sc, WHOLE["s"], 1, WHOLE, ARRIVAL[3], 2)
+    products(0, plan, own, 4)
+    products(1, WHOLE, ARRIVAL[3], 2)
 
-    def pack(name, a, e, tile):
-        wait(v, "l_" + name, 16)
-        inc(v.quantize_mx(T.co[:, a:e], T.so[:, a:e], tile), "q_" + name)
-
-    own = (0, 1, 2, 3)
-
-    pack("ky", K0, R0, T.kyb[:])
-    pack("rt", R0, Q0, T.rtb[:])
-    offsets(0, T.kpo, ("l_kp", 16))
-    elementwise(v, VECTOR[:2], 0, own, 4)
-    pack("qx", Q0, V0, T.qxb[:])
-    elementwise(v, VECTOR[2:V_PACK], 0, own, 4)
-    pack("vv", V0, W, T.vvb[:])
-    elementwise(v, VECTOR[V_PACK:], 0, own, 4)
-    offsets(1, T.kpr, ("r_kp", len(out)))
-    elementwise(v, VECTOR, 1, ARRIVAL, 2)
-
-    elementwise(sc, SCALAR, 0, own, 4)
-    elementwise(sc, SCALAR, 1, ARRIVAL, 2)
-
-    free = {}
-
-    def value(d, h):
-        part = "az"[h]
+    ybank = {"a": BANKS[2], "z": BANKS[3]}
+    for part in "az":
+        ds = [d for d, x in VALUES if x == part]
+    order = {part: [d for d, x in VALUES if x == part] for part in "az"}
+    for d, part in VALUES:
         a, e = PARTS[part]
+        n = e - a
         if d == 0:
-            vc, vs, events = T.co[:, V0:W], T.so[:, V0:W], [("q_vv", 1)] + free[BANKS[2 + h]]
+            vc, vs, events = T.co[:, V0:W], T.so[:, V0:W], [("q_vv", 1)]
         else:
-            vc, vs, events = T.cv[:, 128 * d - 128:128 * d], T.sv[:, 128 * d - 128:128 * d], [("r_v%d" % d, sum(len(out) // len(x[2]) for x in V_BY if d in x[2]))]
-        if d % 4 == 0:
-            ac, as_, events = T["ac%d" % (d // 4)], T["as%d" % (d // 4)], events + [(x, 1) for x in made("qa", d // 4, None, part)]
+            vc, vs, events = T.cv[:, 128 * d - 128:128 * d], T.sv[:, 128 * d - 128:128 * d], [
+                (x, landed[x]) for x in ("r_vc%d" % d, "r_vs%d" % d, "h_VC", "h_VS") if x in landed]
+        if d == 4 or (d, part) == (0, "z") or (d == 0 and not SHARE):
+            ac, as_, events = T["ac%d" % (d // 4)], T["as%d" % (d // 4)], events + [(x, 1) for x in made(WHOLE if d else plan, d // 4, "qa", 0, part)]
         else:
-            ac, as_, events = T.ca, T.sa, events + [("r_a%d%s" % (d, x), 2 * len(every)) for x in packs if meet(x, part)]
-            a, e = a + TQ * (d - 1), e + TQ * (d - 1)
-        for event in events:
+            packs = [s[2] for s in WHOLE["v"] if s[0] == "qa" and meet(PARTS[s[2]], (a, e))] if d else ["a"]
+            ac, as_, events = T.ca, T.sa, events + [("r_a%d%s" % (d, x), 2 * A_LANES[d]) for x in packs]
+            a, e = a + TQ * d, e + TQ * d
+        for event in events + (free[ybank[part]] if d == order[part][0] else []):
             wait(pe, *event)
-        ins = pe.matmul_mx(T[BANKS[2 + h]][:, 0:HALF], vc, vs, ac[:, a:e], as_[:, a:e], d == 0, d == 3)
-        if d == 3:
-            inc(ins, "m_y%d" % h)
+        ins = pe.matmul_mx(T[ybank[part]][:, 0:n], vc, vs, ac[:, a:e], as_[:, a:e], d == order[part][0], d == order[part][-1])
+        if d == order[part][-1]:
+            inc(ins, "m_y" + part)
 
-    products(0, sorted(TENSOR), T.co, T.so, own, 4, [[("q_ky", 1)]] * 4, [("q_rt", 1)], [("q_qx", 1)], free)
-    products(1, TENSOR, T.ck, T.sk, ARRIVAL, 2, arrived, [], [], free)
-    for d, h in VALUES:
-        value(d, h)
-
-    wait(sc, "m_y0")
-    inc(sc.activation(T.ysb[:, 0:HALF], T[BANKS[2]][:, 0:HALF], ActivationFunctionType.Copy), "c_y0")
-    wait(sc, "c_y0")
-    inc(sc.dma_start(T.y[:, 0:HALF], T.ysb[:, 0:HALF]), "st0", 16)
-    wait(v, "m_y1")
-    inc(v.tensor_copy(T.ysb[:, HALF:TQ], T[BANKS[3]][:, 0:HALF]), "c_y1")
-    wait(sy, "c_y1")
-    inc(sy.dma_start(T.y[:, HALF:TQ], T.ysb[:, HALF:TQ]), "st1", 16)
-    wait(sc, "st0", 16)
-    wait(sy, "st1", 16)
-
-
-VALUES = [(0, 0), (0, 1)] + [(_d, _h) for _h in range(2) for _d in (4, 1, 2, 3)]
+    wait(sc, "m_ya")
+    inc(sc.activation(T.ysb[:, 0:CUT], T[ybank["a"]][:, 0:CUT], ActivationFunctionType.Copy), "c_ya")
+    wait(sc, "c_ya")
+    inc(sc.dma_start(T.y[:, 0:CUT], T.ysb[:, 0:CUT]), "sta", 16)
+    wait(v, "m_yz")
+    inc(v.tensor_copy(T.ysb[:, CUT:TQ], T[ybank["z"]][:, 0:TQ - CUT]), "c_yz")
+    wait(sy, "c_yz")
+    inc(sy.dma_start(T.y[:, CUT:TQ], T.ysb[:, CUT:TQ]), "stz", 16)
+    wait(sc, "sta", 16)
+    wait(sy, "stz", 16)

from concourse.bass import DstId, RemoteDMATransfer
from concourse.mybir import dt, AluOpType, ActivationFunctionType

N = 5
TQ = 384
RT = 256
CUT = 256
K0, R0, Q0, V0, W = 0, 512, 512 + RT, 512 + RT + TQ, 512 + RT + TQ + 128

SCRATCH = {
    "kyb": ("sbuf", [128, 2048], "bfloat16"),
    "qxb": ("sbuf", [128, 4 * TQ], "bfloat16"),
    "rtb": ("sbuf", [128, 4 * RT], "bfloat16"),
    "vvb": ("sbuf", [128, 512], "bfloat16"),
    "co": ("sbuf", [128, W], "float8_e4m3fn_x4"),
    "so": ("sbuf", [128, W], "uint8"),
    "ck": ("sbuf", [128, 512], "float8_e4m3fn_x4"),
    "sk": ("sbuf", [128, 512], "uint8"),
    "cv": ("sbuf", [128, 512], "float8_e4m3fn_x4"),
    "sv": ("sbuf", [128, 512], "uint8"),
    "ca": ("sbuf", [128, 4 * TQ], "float8_e4m3fn_x4"),
    "sa": ("sbuf", [128, 4 * TQ], "uint8"),
    "pd": ("dram", [224, 4], "int32"),
    "kh": ("dram", [128, 4], "int32"),
    "qh": ("dram", [128, 4], "int32"),
    "qr": ("sbuf", [128, 24], "int32"),
    "ysb": ("sbuf", [128, TQ], "float32"),
}
BANKS = ["b%d" % _i for _i in range(8)]
for _n in BANKS:
    SCRATCH[_n] = ("psum", [128, 512], "float32")
for _u in range(2):
    SCRATCH["kp%d" % _u] = ("sbuf", [128, 4], "int32")
    SCRATCH["kf%d" % _u] = ("sbuf", [128, 4], "float32")
    SCRATCH["off%d" % _u] = ("sbuf", [128, 96], "uint16")
    SCRATCH["pw%d" % _u] = ("sbuf", [128, 4 * RT], "float32")
    SCRATCH["pk%d" % _u] = ("sbuf", [128, 4 * TQ], "float32")
    SCRATCH["at%d" % _u] = ("sbuf", [128, 4 * TQ], "bfloat16")
    SCRATCH["ac%d" % _u] = ("sbuf", [128, TQ], "float8_e4m3fn_x4")
    SCRATCH["as%d" % _u] = ("sbuf", [128, TQ], "uint8")

PARTS = {"a": (0, CUT), "z": (CUT, TQ), "w": (0, TQ)}
WHOLE = {
    "v": [("cp", 1), ("cp", 2), ("ad", 0, "w"), ("ad", 1, "w"), ("rl", 0, "w"), ("ad", 2, "a"), ("rl", 1, "a"), ("ad", 3, "a"),
          ("rl", 2, "a"), ("rl", 3, "a"), ("qa", 0, "a"), ("ad", 2, "z"), ("ad", 3, "z"), ("rl", 3, "z"), ("qa", 0, "z")],
    "s": [("cp", 0), ("pk", 0, "w"), ("pk", 1, "w"), ("cp", 3), ("pk", 2, "a"), ("pk", 3, "a"), ("pk", 2, "z"), ("pk", 3, "z"),
          ("rl", 1, "z"), ("rl", 2, "z")],
    "p": [("mp", 0), ("mp", 1), ("mp", 2), ("ms", 0, "w"), ("ms", 1, "w"), ("mp", 3), ("ms", 2, "w"), ("ms", 3, "w")],
}


def one_part(x):
    return {"v": [("cp", 1), ("cp", 3)] + [("ad", i, x) for i in range(4)] + [("rl", 2, x), ("rl", 3, x), ("qa", 0, x)],
            "s": [("cp", 0), ("pk", 0, x), ("pk", 1, x), ("cp", 2), ("pk", 2, x), ("pk", 3, x), ("rl", 0, x), ("rl", 1, x)],
            "p": [("mp", i) for i in range(4)] + [("ms", i, x) for i in range(4)]}


MACHINE = 96
WORKERS = ["H0", "H1", "H2", "R"]
SHARE = "G3"
ARRIVAL = (2, 3, 0, 1)
SHARED = (2, 3, 0, 1)

PIECES = {"k0": (True, 0, 128), "k1": (True, 128, 256), "k2": (True, 256, 384), "k3": (True, 384, 512), "ks": (False, K0, R0),
          "rt": (True, R0, Q0), "xs": (False, R0, V0), "qx": (True, Q0, V0), "xa": (True, Q0, Q0 + CUT),
          "r0": (True, R0, R0 + 128), "r1": (True, R0 + 128, Q0), "xz": (True, Q0 + CUT, V0), "rs": (False, R0, Q0), "qs": (False, Q0, V0), "vc": (True, V0, W), "vs": (False, V0, W)}
ALL4 = (1, 2, 3, 4)
SENDS = {
    "R": [[("kp", ("H2", "G1", "H0", "G0", "G3"), 0, 8), ("qp", ("H0", "H1", "H2", "G3"), 8, 16)],
          [("ks", ALL4, 0, 8)],
          [("k2", ("G1",), 8, 12), ("k0", ("G0",), 12, 16)], [("k3", ("H0",), 8, 12), ("k1", ("H2",), 12, 16)],
          [("rt", ("H0",), 8, 16)], [("xs", ("H0", "H1", "H2"), 8, 16)], [("qx", ("H0", "H1", "H2"), 0, 16)],
          [("ks", ("G3",), 0, 16)],
          [("vc", ("G0", "G1"), 0, 16)], [("vs", ("G2",), 0, 16)]],
    "H0": [[("kp", (3,), 0, 8)], [("k3", ALL4, 0, 8)], [("rt", ("H1", "H2", "G3"), 8, 16)], [("k3", ("G3",), 8, 16)]],
    "H1": [[("xs", ("G3",), 0, 16)], [("xa", ("G3",), 0, 16)]],
    "H2": [[("kp", (1,), 0, 8)], [("k1", ALL4, 0, 8)], [("k1", ("G3",), 8, 16)]],
    "G0": [[("kp", (4,), 0, 8)], [("k0", ALL4, 0, 8)], [("k0", ("G3",), 8, 16)], [("vc", (1,), 0, 4), ("vc", (2,), 4, 8)]],
    "G1": [[("kp", (2,), 0, 8)], [("k2", ALL4, 0, 8)], [("k2", ("G3",), 8, 16)], [("vc", (3,), 0, 4), ("vc", (4,), 4, 8)]],
    "G2": [[("vs", (d,), 2 * d - 2, 2 * d) for d in ALL4]],
    "G3": [],
}
LOADS = [("y", "ky", None), ("y", "pos", None), ("s", "rt", ("l_pos", 32)), ("y", "qx", None), ("y", "vv", ("q_rt", 1))]
R_VECTOR = ["ky", "of", "rt", "qx", 2, "vv"]
VALUES = [(0, "z"), (0, "a"), (1, "a"), (2, "a"), (4, "a"), (3, "a"), (1, "z"), (2, "z"), (4, "z"), (3, "z")]

H = ("H0", "H1", "H2")
WHOLE = {"v": [("cp", 1), ("pk", 1, "w"), ("ad", 0, "w"), ("cp", 3), ("ad", 1, "w"), ("ad", 2, "w"), ("rl", 1, "a"), ("ad", 3, "a"), ("rl", 3, "a"),
               ("qa", 0, "a"), ("ad", 3, "z"), ("rl", 3, "z"), ("qa", 0, "z")],
         "s": [("cp", 0), ("pk", 0, "w"), ("cp", 2), ("pk", 2, "w"), ("pk", 3, "a"), ("rl", 0, "w"), ("rl", 2, "a"), ("pk", 3, "z"), ("rl", 2, "z"),
               ("rl", 1, "z")],
         "p": [("mp", 0), ("mp", 1), ("ms", 0, "w"), ("ms", 1, "w"), ("mp", 2), ("mp", 3), ("ms", 2, "w"), ("ms", 3, "w")]}
SHARE = None
A_LANES = [16, 16, 16, 16]
V_TO = {"vc": "R", "vs": "R"}
ARRIVAL = [(2, 3, 0, 1)] * 4
LOADS = [("y", "ky", None), ("y", "rt", None), ("y", "pos", None), ("s", "qx", ("l_pos", 32)), ("s", "vv", None)]
SENDS = {
    "R": [[("kp", ("G1", "H0", "H2", "G0"), 0, 2)], [("qp", ("H0",), 8, 16), ("qp", ("H1",), 4, 8), ("qp", ("H2",), 2, 4)],
          [("ks", ALL4, 0, 8), ("k2", ("G1",), 8, 12), ("k3", ("H0",), 12, 16)],
          [("r0", ("H2",), 8, 12), ("r1", ("H0",), 12, 16)],
          [("k0", ("G0",), 8, 12), ("k1", ("H2",), 12, 16)],
          [("xs", H, 8, 16)], [("qx", ("H0", "H1"), 0, 8), ("qx", ("H2",), 8, 16)],
          [("vc", ("G0", "G1"), 0, 16)], [("vs", ("G1", "H1"), 0, 16)]],
    "H0": [[("kp", (3,), 0, 8)], [("k3", ALL4, 0, 8)], [("r1", ("H1", "H2"), 8, 16)]],
    "H1": [[("vs", (1,), 0, 4), ("vs", (2,), 4, 8)]],
    "H2": [[("kp", (1,), 0, 8)], [("r0", ("H0", "H1"), 8, 16)], [("k1", ALL4, 0, 8)]],
    "G0": [[("kp", (4,), 0, 8)], [("k0", ALL4, 0, 8)], [("vc", (1,), 0, 4), ("vc", (2,), 4, 8)]],
    "G1": [[("kp", (2,), 0, 8)], [("k2", ALL4, 0, 8)], [("vc", (3,), 0, 4), ("vc", (4,), 4, 8)], [("vs", (3,), 0, 4), ("vs", (4,), 4, 8)]],
}
R_VECTOR = ["ky", "rt", "of", "qx", 2, "vv"]
VALUES = [(0, "a"), (0, "z"), (1, "a"), (1, "z"), (4, "a"), (2, "a"), (4, "z"), (3, "a"), (2, "z"), (3, "z")]

SEMAPHORES = ["l_ky", "l_rt", "l_qx", "l_vv", "l_kp", "l_qp", "l_pos", "q_ky", "q_rt", "q_qx", "q_vv",
              "sent", "m_ya", "m_yz", "c_ya", "c_yz", "sta", "stz", "kf0", "kf1", "of0", "of1"]
SEMAPHORES += ["h_" + _p for _p in list(PIECES) + ["kp", "qp", "VC", "VS"]] + ["r_k" + _p for _p in "0123sp"]
SEMAPHORES += ["r_%s%d" % (_p, _d) for _p in ("vc", "vs") for _d in ALL4] + ["r_a%d%s" % (_d, _x) for _d in range(4) for _x in "azw"]


def label(u, step):
    return "%s%d%d%s" % (step[0], u, step[1], "".join(step[2:]))


SEMAPHORES += sorted({label(_u, _s) for _u, _plan in ((0, WHOLE), (1, WHOLE)) for _q in _plan.values() for _s in _q})


def bits(es):
    return sum(1 << e for e in es)


def team(rank_core, topo):
    names = {"R": rank_core}
    mate = [c for c in range(MACHINE) if topo.mates(topo.chip(c), topo.chip(rank_core)) and topo.may_write(c, rank_core)]
    others = sorted((c for c in topo.cores_of(rank_core) if c != rank_core), key=lambda c: topo.may_write(c, mate[0]))
    for letters, group in (("HG", others), ("MF", mate)):
        for letter, same in zip(letters, (True, False)):
            for i, c in enumerate([c for c in group if (topo.die(c) == topo.die(rank_core)) == same]):
                names["%s%d" % (letter, i)] = c
    return names


def meet(p, q):
    return p[0] < q[1] and q[0] < p[1]


def rank_program(g, core, T, topo):
    v, sc, pe, sy = g.vector, g.scalar, g.tensor, g.sync
    cores = list(T.cores)
    teams = [team(c, topo) for c in cores]
    found = [(i, name) for i, t in enumerate(teams) for name, c in t.items() if c == core]
    if not found:
        return
    r, role = found[0]
    me, mine = cores[r], teams[r]
    out = topo.engines(me, cores[(r + 1) % N])
    every = out + [e for e in topo.engines(me, mine["H0"]) if e not in out]
    sent = [0]
    waited = set()

    def wait(queue, name, n=1):
        key = ([q is queue for q in (g, v, sc, pe, sy)].index(True), name, n)
        if key not in waited:
            waited.add(key)
            queue.wait_ge(T.sem[name], n)

    def inc(ins, name, n=1):
        ins.then_inc(T.sem[name], n)

    def move(dsts, there, src, sem, es):
        ids = []
        for c in dsts:
            a = topo.addr(c)
            ids.append(DstId(rid=a[0], pnc=a[1]))
        sent[0] += len(es)
        return RemoteDMATransfer(dst_ids=ids, dma_engine_mask=bits(es), remote_sem=T.sem[sem], srcs=[src], dsts=[there] * len(dsts))

    def send(*moves):
        g.remote_dma_fused(list(moves), local_sem=T.sem["sent"])

    def run(codes, plane, is_codes, a, e):
        return codes[:, a:e].bitcast(dt.uint8) if is_codes else plane[:, a:e]

    def name_of(p, to):
        return to if to in mine else V_TO[p] if p[0] == "v" else WORKERS[to - 1]

    def sem_of(p, to):
        return "h_" + p if to in mine else "r_%s%d" % (p, to) if p[0] == "v" else "r_" + p

    landed = {sem_of(p, to): e - a for calls in SENDS.values() for c in calls for p, tos, a, e in c for to in tos if name_of(p, to) == role}

    def here(is_codes, a, e):
        if role == "R":
            return [("q_" + n, 1) for n, span in (("ky", (K0, R0)), ("rt", (R0, Q0)), ("qx", (Q0, V0)), ("vv", (V0, W))) if meet(span, (a, e))]
        return [("h_" + p, landed["h_" + p]) for p, x in PIECES.items() if "h_" + p in landed and x[0] == is_codes and meet(x[1:], (a, e))]

    def transfer(p, tos, first, end):
        far = tos[0] not in mine
        dsts = [teams[(r + to) % N][name_of(p, to)] if far else mine[to] for to in tos]
        if p in PIECES:
            c, a, e = PIECES[p]
            events, src = here(c, a, e), run(T.co, T.so, c, a, e)
            there = src if not far else run(T.cv, T.sv, c, 128 * tos[0] - 128, 128 * tos[0]) if p[0] == "v" else run(T.ck, T.sk, c, a, e)
        elif p in ("VC", "VS"):
            events = [(x, landed[x]) for x in ["r_%s%d" % (p.lower(), d) for d in ALL4]]
            src = there = run(T.cv, T.sv, p == "VC", 0, 512)
        elif role == "R":
            events, src, there = [("l_pos", 32)], T.pd[0:128, :] if p == "kp" else T.pd[96:224, :], T.kh[:] if p == "kp" else T.qh[:]
        elif p == "kp":
            events, src, there = [("h_kp", landed["h_kp"])], T.kh[:], T.kp1[:]
        else:
            events, src, there = [("h_qp", landed["h_qp"])], T.qh[:], T.qh[:]
        for event in events:
            wait(g, *event)
        return move(dsts, there, src, sem_of(p, tos[0]), every[first:end])

    for c in SENDS.get(role, []):
        send(*[transfer(*x) for x in c])

    def offsets(u, kp_event):
        kf, off = T["kf%d" % u], T["off%d" % u]
        wait(v, *kp_event)
        inc(v.tensor_scalar(kf[:], T["kp%d" % u][:], 128.0, None, AluOpType.subtract), "kf%d" % u)
        wait(v, "l_qp", 128)
        wait(v, "kf%d" % u)
        for b in range(4):
            inc(v.tensor_scalar(off[:, 24 * b:24 * b + 24], T.qr[:], kf[:, b:b + 1], RT - 1.0, AluOpType.subtract, AluOpType.min), "of%d" % u)

    def made(plan, u, kind, i, part):
        return [label(u, s) for s in plan["v"] + plan["s"] + plan["p"] if s[0] == kind and i in (None, s[1]) and meet(PARTS[s[2]], PARTS[part])]

    free = {}

    def products(u, plan, order, pbanks):
        kc, ks = (T.ck, T.sk) if u else (T.co, T.so)
        for step in plan["p"]:
            i = step[1]
            b = order[i]
            if step[0] == "mp":
                bank, a, e, after = BANKS[i % pbanks], R0, Q0, [label(u, ("cp", i))]
            else:
                bank, a, e, after = BANKS[4 + i], Q0 + PARTS[step[2]][0], Q0 + PARTS[step[2]][1], made(plan, u, "ad", i, "w")
            keys = [(x, landed[x]) for x in ("r_ks", "r_k%d" % b)] if u else here(False, K0, R0) + here(True, 128 * b, 128 * b + 128)
            for event in keys + here(False, a, e) + here(True, a, e) + free.get(bank, []):
                wait(pe, *event)
            inc(pe.matmul_mx(T[bank][:, 0:e - a], kc[:, 128 * b:128 * b + 128], ks[:, 128 * b:128 * b + 128],
                             T.co[:, a:e], T.so[:, a:e], True, True), label(u, step))
            free[bank] = [(x, 1) for x in after]

    def elementwise(queue, steps, u, plan, order, pbanks):
        tile, pw, pk, off = T["at%d" % u], T["pw%d" % u], T["pk%d" % u], T["off%d" % u]
        first = PARTS[plan["p"][-1][2]][0]
        for step in steps:
            kind, i = step[:2]
            b = order[i]
            window = pw[:, RT * b:RT * b + RT]
            if kind == "cp":
                wait(queue, label(u, ("mp", i)))
                bank = T[BANKS[i % pbanks]][:, 0:RT]
                inc(v.tensor_copy(window, bank) if queue is v else sc.activation(window, bank, ActivationFunctionType.Copy), label(u, step))
                continue
            a, e = PARTS[step[2]]
            picked, col = pk[:, TQ * b + a:TQ * b + e], tile[:, 4 * a + b:4 * e:4]
            if kind == "pk":
                wait(queue, "of%d" % u, 4)
                needs = [label(u, ("cp", i))]
            elif kind == "ad":
                needs = made(plan, u, "ms", i, step[2]) + made(plan, u, "pk", i, step[2])
            elif kind == "rl":
                needs = made(plan, u, "ad", i, step[2])
            else:
                needs = made(plan, u, "rl", None, step[2])
            for x in needs:
                wait(queue, x)
            if kind == "pk":
                pick = window.indirect(off[:, 24 * b + a // 16:24 * b + e // 16])
                ins = v.tensor_copy(picked, pick) if queue is v else sc.activation(picked, pick, ActivationFunctionType.Copy)
            elif kind == "ad":
                ins = v.tensor_tensor(col, T[BANKS[4 + i]][:, a - first:e - first], picked, AluOpType.add)
            elif kind == "qa":
                ins = v.quantize_mx(T["ac%d" % u][:, a:e], T["as%d" % u][:, a:e], tile[:, 4 * a:4 * e])
            elif queue is v:
                ins = v.tensor_scalar(col, col, 0.0, 0.03125, AluOpType.max, AluOpType.mult)
            else:
                ins = sc.activation(col, col, ActivationFunctionType.Relu, scale=0.03125)
            inc(ins, label(u, step))

    def repeat(table, queues, event=None):
        for q in range(8):
            queue = queues[q % len(queues)]
            if event:
                wait(queue, *event)
            inc(queue.dma_start(T.qr[16 * q:16 * q + 16, :], table), "l_qp", 16)

    if role in WORKERS[:3] or role == SHARE:
        u, d, plan, order = (0, 0, one_part("a"), SHARED) if role == SHARE else (1, WORKERS.index(role) + 1, WHOLE, ARRIVAL[WORKERS.index(role)])
        if role == SHARE:
            wait(sy, "h_kp", landed["h_kp"])
            inc(sy.dma_start(T.kp0[:], T.kh[:]), "l_kp", 16)
        repeat(T.qh[32:128, :], (sy, sc), ("h_qp", landed["h_qp"]))
        offsets(u, ("r_kp", landed["r_kp"]) if u else ("l_kp", 16))
        products(u, plan, order, 4)
        elementwise(sc, plan["s"], u, plan, order, 4)
        elementwise(v, plan["v"], u, plan, order, 4)
        for step in plan["v"]:
            if step[0] == "qa":
                wait(g, label(u, step))
                a, e = PARTS[step[2]]
                for c in (True, False):
                    send(move([me], run(T.ca, T.sa, c, TQ * d + a, TQ * d + e), run(T["ac%d" % u], T["as%d" % u], c, a, e),
                              "r_a%d%s" % (d, step[2]), every[:A_LANES[d]]))
    if sent[0]:
        wait(g, "sent", sent[0])
    if role != "R":
        return

    inc(sy.dma_start(T.pd[0:128, :], T.kp[:]), "l_pos", 16)
    inc(sc.dma_start(T.pd[128:224, :], T.qp[:]), "l_pos", 16)
    tiles = {"ky": (K0, R0, T.kyb, T.ky), "rt": (R0, Q0, T.rtb, T.rt), "qx": (Q0, V0, T.qxb, T.qx), "vv": (V0, W, T.vvb, T.vv)}
    for key, what, event in LOADS:
        queue = sy if key == "y" else sc
        if event:
            wait(queue, *event)
        if what == "pos":
            inc(queue.dma_start(T.kp0[:], T.kp[:]), "l_kp", 16)
            repeat(T.qp[:], (queue,))
        else:
            inc(queue.dma_start(tiles[what][2][:], tiles[what][3][:]), "l_" + what, 16)

    own, plan = (0, 1, 2, 3), one_part("z") if SHARE else dict(WHOLE, p=sorted(WHOLE["p"]))
    done = 0
    for x in R_VECTOR:
        if x == "of":
            offsets(0, ("l_kp", 16))
        elif x in tiles:
            a, e, tile, _ = tiles[x]
            wait(v, "l_" + x, 16)
            inc(v.quantize_mx(T.co[:, a:e], T.so[:, a:e], tile[:]), "q_" + x)
        else:
            elementwise(v, plan["v"][done:x], 0, plan, own, 4)
            done = x
    elementwise(v, plan["v"][done:], 0, plan, own, 4)
    offsets(1, ("r_kp", landed["r_kp"]))
    elementwise(v, WHOLE["v"], 1, WHOLE, ARRIVAL[3], 2)
    elementwise(sc, plan["s"], 0, plan, own, 4)
    elementwise(sc, WHOLE["s"], 1, WHOLE, ARRIVAL[3], 2)
    products(0, plan, own, 4)
    products(1, WHOLE, ARRIVAL[3], 2)

    ybank = {"a": BANKS[2], "z": BANKS[3]}
    for part in "az":
        ds = [d for d, x in VALUES if x == part]
    order = {part: [d for d, x in VALUES if x == part] for part in "az"}
    for d, part in VALUES:
        a, e = PARTS[part]
        n = e - a
        if d == 0:
            vc, vs, events = T.co[:, V0:W], T.so[:, V0:W], [("q_vv", 1)]
        else:
            vc, vs, events = T.cv[:, 128 * d - 128:128 * d], T.sv[:, 128 * d - 128:128 * d], [
                (x, landed[x]) for x in ("r_vc%d" % d, "r_vs%d" % d, "h_VC", "h_VS") if x in landed]
        if d == 4 or (d, part) == (0, "z") or (d == 0 and not SHARE):
            ac, as_, events = T["ac%d" % (d // 4)], T["as%d" % (d // 4)], events + [(x, 1) for x in made(WHOLE if d else plan, d // 4, "qa", 0, part)]
        else:
            packs = [s[2] for s in WHOLE["v"] if s[0] == "qa" and meet(PARTS[s[2]], (a, e))] if d else ["a"]
            ac, as_, events = T.ca, T.sa, events + [("r_a%d%s" % (d, x), 2 * A_LANES[d]) for x in packs]
            a, e = a + TQ * d, e + TQ * d
        for event in events + (free[ybank[part]] if d == order[part][0] else []):
            wait(pe, *event)
        ins = pe.matmul_mx(T[ybank[part]][:, 0:n], vc, vs, ac[:, a:e], as_[:, a:e], d == order[part][0], d == order[part][-1])
        if d == order[part][-1]:
            inc(ins, "m_y" + part)

    wait(sc, "m_ya")
    inc(sc.activation(T.ysb[:, 0:CUT], T[ybank["a"]][:, 0:CUT], ActivationFunctionType.Copy), "c_ya")
    wait(sc, "c_ya")
    inc(sc.dma_start(T.y[:, 0:CUT], T.ysb[:, 0:CUT]), "sta", 16)
    wait(v, "m_yz")
    inc(v.tensor_copy(T.ysb[:, CUT:TQ], T[ybank["z"]][:, 0:TQ - CUT]), "c_yz")
    wait(sy, "c_yz")
    inc(sy.dma_start(T.y[:, CUT:TQ], T.ysb[:, CUT:TQ]), "stz", 16)
    wait(sc, "sta", 16)
    wait(sy, "stz", 16)
